import numpy as np
import ml_dtypes


def mxq(x, axis, fmt="e4m3"):
    dtype, down = {"e4m3": (ml_dtypes.float8_e4m3fn, 7), "e5m2": (ml_dtypes.float8_e5m2, 14)}[fmt]
    v = np.moveaxis(np.asarray(x, np.float32).astype(ml_dtypes.bfloat16).astype(np.float64), axis, -1)
    blocks = v.reshape(v.shape[:-1] + (-1, 32))
    amax = np.abs(blocks).max(-1, keepdims=True)
    byte = np.maximum(np.where(amax > 0, np.frexp(amax)[1] - 1 + 127, 0) - down, 1)
    scale = np.exp2(byte - 127.0)
    codes = (blocks / scale).astype(np.float32).astype(dtype).astype(np.float64)
    return np.moveaxis((codes * scale).reshape(v.shape), -1, axis)


WIDE = False


def mx_kscale(k):
    if not WIDE:
        return np.ones(k)
    levels = np.array([10, -10, 5, -5, 0])
    if k % 512:
        return np.exp2(np.random.permutation(np.resize(levels, k // 32))).repeat(32)
    a = np.empty((k // 512, 16))
    for p in range(k // 512):
        a[p, :8] = np.random.permutation(np.resize(levels, 8))
        for g in range(8):
            far = levels[np.abs(levels - a[p, g]) >= 10]
            a[p, g + 8] = far[np.random.randint(len(far))]
    return np.exp2(a.ravel()).repeat(32)


def f64(x):
    return np.asarray(x).astype(np.float64)


def striped(idx):
    return np.tile(idx.reshape(-1, 16).T, (8, 1)).astype(np.uint16)


def unstriped(offs):
    return offs[:16].T.reshape(-1).astype(np.int64)


def striped8(idx):
    return np.concatenate([x.reshape(-1, 16).T for x in idx]).astype(np.uint16)


def runs(offs, k):
    lists = np.stack([offs[16 * r : 16 * r + 16].T.reshape(-1) for r in range(8)]).astype(np.int64)
    return lists[np.arange(k) % 512 // 64]


def pack_weight(w):
    k, n = w.shape
    w = f64(np.asarray(w, np.float32).astype(ml_dtypes.bfloat16)).reshape(k // 32, 32, n)
    amax = np.abs(w).max(1)
    byte = np.clip(np.where(amax > 0, np.frexp(amax)[1] - 1 + 127 - 7, 1), 1, 254)
    scaled = (w * np.exp2(127.0 - byte)[:, None, :]).reshape(k, n).astype(np.float32)
    words = np.ascontiguousarray(scaled.reshape(k // 512, 128, 4, n).transpose(0, 1, 3, 2)).astype(ml_dtypes.float8_e4m3fn).view(np.uint8)
    return words, np.ascontiguousarray(byte.astype(np.uint8).reshape(k // 512, 16, n))


def unpack_weight(words, scales):
    g, p, n, _ = words.shape
    vals = np.ascontiguousarray(words).view(ml_dtypes.float8_e4m3fn).astype(np.float64) * np.repeat(np.exp2(scales.astype(np.float64) - 127.0), 8, axis=1)[..., None]
    return vals.transpose(0, 1, 3, 2).reshape(g * 512, n)


def sigmoid(v):
    return 1.0 / (1.0 + np.exp(-np.maximum(v, -700.0)))


K, T, S, N = 512, 2048, 512, 512


def setup_inputs():
    n = np.random.standard_normal
    s = mx_kscale(K)[:, None]
    packed_xT = pack_weight(n((K, T)) * s)
    return {
        "x_words": packed_xT[0],
        "x_scales": packed_xT[1],
        "w1": (n((K, N)) / np.sqrt(K) / s).astype(np.float32),
        "dg1": np.random.uniform(0.1, 1.0, (N, S)).astype(np.float32),
        "dg2": np.random.uniform(0.1, 1.0, (N, S)).astype(np.float32),
        "offs": striped(np.random.permutation(T)[:S]),
        "p1": striped8(np.stack([np.random.permutation(S) for _ in range(8)])),
        "p2": striped8(np.stack([np.random.permutation(S) for _ in range(8)])),
    }


def reference(x_words, x_scales, w1, dg1, dg2, offs, p1, p2):
    xq = unpack_weight(x_words, x_scales)[:, unstriped(offs)]
    y = mxq(f64(w1), 0, "e4m3").T @ xq
    return f64(dg1) * (sigmoid(y[np.arange(N)[:, None], runs(p1, N)] - y)) + f64(dg2) * (sigmoid(y[np.arange(N)[:, None], runs(p2, N)] - y))

@@ -1,0 +1,132 @@
+from contextlib import ExitStack
+
+import concourse.mybir as mybir
+
+F32 = mybir.dt.float32
+BF16 = mybir.dt.bfloat16
+I32 = mybir.dt.int32
+U32 = mybir.dt.uint32
+U16 = mybir.dt.uint16
+U8 = mybir.dt.uint8
+FP8X4 = mybir.dt.float8_e4m3fn_x4
+ALU = mybir.AluOpType
+ACT = mybir.ActivationFunctionType
+
+P = 128
+K, T, S, N = 512, 2048, 512, 512
+TILES = N // P
+HALF = S // 2
+FLOPS = 2 * K * N * S
+
+
+def tile_picked_lamrank_none_p_kernel(tc, x_words, x_scales, w1, dg1, dg2, offs, p1, p2, out):
+    nc = tc.nc
+    with ExitStack() as ctx:
+        keep = ctx.enter_context(tc.tile_pool(name="keep", bufs=1))
+        psum = ctx.enter_context(tc.psum_pool(name="psum", bufs=1))
+
+        offs_sb = keep.tile([P, S // 16], U16, name="offs_sb")
+        p1_sb = keep.tile([P, S // 16], U16, name="p1_sb")
+        p2_sb = keep.tile([P, S // 16], U16, name="p2_sb")
+        lists = [p1_sb, p2_sb]
+        w_raw = keep.tile([P, 4, N], F32, name="w_raw")
+        xs_all = keep.tile([P, T], U8, name="xs_all")
+        xw_all = keep.tile([P, T], I32, name="xw_all")
+        warm = keep.tile([P, 8], F32, name="warm")
+        warm2 = keep.tile([P, 8], F32, name="warm2")
+        windows = [keep.tile([P, 2 * S], F32, name="win%d" % t) for t in range(TILES)]
+        gains = [[keep.tile([P, 2, S], F32, name="gain%d_%d" % (l, h)) for h in range(2)] for l in range(2)]
+
+        nc.vector.memset(xs_all[:].bitcast(I32), 0)
+        nc.vector.memset(warm[:], 0.0)
+        nc.scalar.activation(out=warm2[:], in_=warm[:], func=ACT.Sigmoid)
+
+        nc.sync.dma_start(out=w_raw[:], in_=w1.rearrange("(p j) m -> p j m", j=4))
+        for q in range(4):
+            nc.sync.dma_start(out=xs_all[32 * q : 32 * q + 4, :].bitcast(I32), in_=x_scales[0, 4 * q : 4 * q + 4, :].bitcast(I32))
+        nc.sync.dma_start(out=offs_sb[:], in_=offs)
+        nc.sync.dma_start(out=xw_all[:], in_=x_words[0].rearrange("p n t -> p (n t)").bitcast(I32))
+        nc.sync.dma_start(out=p1_sb[:], in_=p1)
+        nc.sync.dma_start(out=p2_sb[:], in_=p2)
+        dgv = [dg1.rearrange("(p t) j -> p t j", t=TILES), dg2.rearrange("(p t) j -> p t j", t=TILES)]
+        for h in range(2):
+            for l in range(2):
+                nc.sync.dma_start(out=gains[l][h][:], in_=dgv[l][:, 2 * h : 2 * h + 2, :])
+        for t in range(TILES):
+            nc.vector.memset(windows[t][:, S:], 0.0)
+
+        w_grp = keep.tile([P, TILES, P, 4], BF16, name="w_grp", align_bytes=64)
+        w_codes = keep.tile([P, N], U32, name="w_codes", align_bytes=64)
+        w_scales = keep.tile([P, N], U8, name="w_scales", align_bytes=64)
+        src = w_raw[:].rearrange("p j (m t) -> p m j t", t=TILES)
+        dst = w_grp[:].rearrange("p t m j -> p m j t")
+        SPLIT = 80
+        nc.vector.tensor_copy(out=dst[:, :SPLIT], in_=src[:, :SPLIT])
+        nc.scalar.copy(out=dst[:, SPLIT:], in_=src[:, SPLIT:])
+
+        xs = keep.tile([P, S], U8, name="xs", align_bytes=64)
+        xw = keep.tile([P, S], U32, name="xw", align_bytes=64)
+        nc.vector.tensor_copy(out=xs[:], in_=xs_all[:].indirect(offs_sb[:]))
+        nc.vector.quantize_mx(out=w_codes[:].bitcast(FP8X4), scales=w_scales[:], in_=w_grp[:].rearrange("p t m j -> p (t m j)"))
+        for h in range(2):
+            nc.vector.tensor_copy(out=xw[:, h * HALF : (h + 1) * HALF], in_=xw_all[:].bitcast(U32).indirect(offs_sb[:, 16 * h : 16 * h + 16]))
+
+        def product(t, acc, cols):
+            nc.tensor.matmul_mx(
+                out=acc,
+                lhsT=w_codes[:, t * P : (t + 1) * P].bitcast(FP8X4),
+                lhsT_scale=w_scales[:, t * P : (t + 1) * P],
+                rhs=xw[:, cols].bitcast(FP8X4),
+                rhs_scale=xs[:, cols],
+                start=True,
+                stop=True,
+            )
+
+        own = [keep.tile([P, S], F32, name="own%d" % t) for t in range(TILES)]
+        diff = [keep.tile([P, 2, S], F32, name="diff%d" % t) for t in range(TILES)]
+        sig = [keep.tile([P, 2, S], F32, name="sig%d" % t) for t in range(TILES)]
+        prod = [keep.tile([P, 2, S], F32, name="prod%d" % t) for t in range(TILES)]
+        res = [keep.tile([P, S], F32, name="res%d" % t) for t in range(TILES)]
+        outv = out.rearrange("(p t) j -> p t j", t=TILES)
+
+        def scores(t, pieces):
+            width = S // pieces
+            for h in range(pieces):
+                cols = slice(h * width, (h + 1) * width)
+                acc = psum.tile([P, width], F32, name="acc%d_%d" % (t, h))
+                product(t, acc[:], cols)
+                nc.scalar.copy(out=windows[t][:, cols], in_=acc[:])
+                nc.scalar.copy(out=own[t][:, cols], in_=acc[:])
+
+        def gather(t, l, pieces):
+            width = S // pieces
+            for h in range(pieces):
+                cols = slice(h * width, (h + 1) * width)
+                o = lists[l][:, h * width // 16 : (h + 1) * width // 16]
+                nc.vector.tensor_tensor(out=diff[t][:, l, cols], in0=windows[t][:].indirect(o), in1=own[t][:, cols], op=ALU.subtract)
+            nc.scalar.activation(out=sig[t][:, l, :], in_=diff[t][:, l, :], func=ACT.Sigmoid)
+
+        def weigh(t, l):
+            nc.vector.tensor_tensor(out=prod[t][:, l, :], in0=sig[t][:, l, :], in1=gains[l][t // 2][:, t % 2, :], op=ALU.mult)
+
+        def finish(t):
+            nc.vector.tensor_tensor(out=res[t][:], in0=prod[t][:, 0, :], in1=prod[t][:, 1, :], op=ALU.add)
+            nc.sync.dma_start(out=outv[:, t, :], in_=res[t][:])
+
+        scores(0, 2)
+        scores(1, 1)
+        gather(0, 0, 2)
+        gather(0, 1, 1)
+        scores(2, 1)
+        scores(3, 1)
+        for t in range(1, TILES):
+            gather(t, 0, 1)
+            weigh(t - 1, 0)
+            gather(t, 1, 1)
+            weigh(t - 1, 1)
+            if t > 1:
+                finish(t - 2)
+        weigh(TILES - 1, 0)
+        finish(TILES - 2)
+        weigh(TILES - 1, 1)
+        finish(TILES - 1)

@@ -1,6 +1,7 @@
 from contextlib import ExitStack
 
 import concourse.mybir as mybir
+from concourse.masks import make_identity
 
 F32 = mybir.dt.float32
 BF16 = mybir.dt.bfloat16
@@ -30,21 +31,23 @@ def tile_picked_lamrank_none_p_kernel(tc, x_words, x_scales, w1, dg1, dg2, offs,
         p2_sb = keep.tile([P, S // 16], U16, name="p2_sb")
         lists = [p1_sb, p2_sb]
         w_raw = keep.tile([P, 4, N], F32, name="w_raw")
-        xs_all = keep.tile([P, T], U8, name="xs_all")
-        xw_all = keep.tile([P, T], I32, name="xw_all")
+        xs_all = keep.tile([P, T], U8, name="xs_all", tag="early", align_bytes=64)
+        xw_all = keep.tile([P, T], I32, name="xw_all", tag="late", align_bytes=64)
         warm = keep.tile([P, 8], F32, name="warm")
         warm2 = keep.tile([P, 8], F32, name="warm2")
+        ident = keep.tile([P, P], F32, name="ident")
         windows = [keep.tile([P, 2 * S], F32, name="win%d" % t) for t in range(TILES)]
         gains = [[keep.tile([P, 2, S], F32, name="gain%d_%d" % (l, h)) for h in range(2)] for l in range(2)]
 
         nc.vector.memset(xs_all[:].bitcast(I32), 0)
         nc.vector.memset(warm[:], 0.0)
         nc.scalar.activation(out=warm2[:], in_=warm[:], func=ACT.Sigmoid)
+        make_identity(nc, ident[:])
 
+        nc.sync.dma_start(out=offs_sb[:], in_=offs)
         nc.sync.dma_start(out=w_raw[:], in_=w1.rearrange("(p j) m -> p j m", j=4))
         for q in range(4):
             nc.sync.dma_start(out=xs_all[32 * q : 32 * q + 4, :].bitcast(I32), in_=x_scales[0, 4 * q : 4 * q + 4, :].bitcast(I32))
-        nc.sync.dma_start(out=offs_sb[:], in_=offs)
         nc.sync.dma_start(out=xw_all[:], in_=x_words[0].rearrange("p n t -> p (n t)").bitcast(I32))
         nc.sync.dma_start(out=p1_sb[:], in_=p1)
         nc.sync.dma_start(out=p2_sb[:], in_=p2)
@@ -55,27 +58,34 @@ def tile_picked_lamrank_none_p_kernel(tc, x_words, x_scales, w1, dg1, dg2, offs,
         for t in range(TILES):
             nc.vector.memset(windows[t][:, S:], 0.0)
 
-        w_grp = keep.tile([P, TILES, P, 4], BF16, name="w_grp", align_bytes=64)
-        w_codes = keep.tile([P, N], U32, name="w_codes", align_bytes=64)
-        w_scales = keep.tile([P, N], U8, name="w_scales", align_bytes=64)
+        w_grp = [keep.tile([P, 2, P, 4], BF16, name="w_grp%d" % h, align_bytes=64) for h in range(2)]
+        w_codes = {}
+        w_scales = [keep.tile([P, 2 * P], U8, name="w_scales%d" % h, align_bytes=64) for h in range(2)]
         src = w_raw[:].rearrange("p j (m t) -> p m j t", t=TILES)
-        dst = w_grp[:].rearrange("p t m j -> p m j t")
-        SPLIT = 80
-        nc.vector.tensor_copy(out=dst[:, :SPLIT], in_=src[:, :SPLIT])
-        nc.scalar.copy(out=dst[:, SPLIT:], in_=src[:, SPLIT:])
+        for h in range(2):
+            nc.scalar.copy(out=w_grp[h][:].rearrange("p t m j -> p m j t"), in_=src[:, :, :, 2 * h : 2 * h + 2])
 
         xs = keep.tile([P, S], U8, name="xs", align_bytes=64)
         xw = keep.tile([P, S], U32, name="xw", align_bytes=64)
-        nc.vector.tensor_copy(out=xs[:], in_=xs_all[:].indirect(offs_sb[:]))
-        nc.vector.quantize_mx(out=w_codes[:].bitcast(FP8X4), scales=w_scales[:], in_=w_grp[:].rearrange("p t m j -> p (t m j)"))
-        for h in range(2):
+
+        def quantize(h, tag):
+            w_codes[h] = keep.tile([P, 2 * P], U32, name="w_codes%d" % h, tag=tag, align_bytes=64)
+            nc.vector.quantize_mx(out=w_codes[h][:].bitcast(FP8X4), scales=w_scales[h][:], in_=w_grp[h][:].rearrange("p t m j -> p (t m j)"))
+
+        def pick(h):
             nc.vector.tensor_copy(out=xw[:, h * HALF : (h + 1) * HALF], in_=xw_all[:].bitcast(U32).indirect(offs_sb[:, 16 * h : 16 * h + 16]))
+
+        nc.vector.tensor_copy(out=xs[:], in_=xs_all[:].indirect(offs_sb[:]))
+        quantize(0, "early")
+        pick(0)
+        pick(1)
+        quantize(1, "late")
 
         def product(t, acc, cols):
             nc.tensor.matmul_mx(
                 out=acc,
-                lhsT=w_codes[:, t * P : (t + 1) * P].bitcast(FP8X4),
-                lhsT_scale=w_scales[:, t * P : (t + 1) * P],
+                lhsT=w_codes[t // 2][:, t % 2 * P : (t % 2 + 1) * P].bitcast(FP8X4),
+                lhsT_scale=w_scales[t // 2][:, t % 2 * P : (t % 2 + 1) * P],
                 rhs=xw[:, cols].bitcast(FP8X4),
                 rhs_scale=xs[:, cols],
                 start=True,
@@ -84,49 +94,91 @@ def tile_picked_lamrank_none_p_kernel(tc, x_words, x_scales, w1, dg1, dg2, offs,
 
         own = [keep.tile([P, S], F32, name="own%d" % t) for t in range(TILES)]
         diff = [keep.tile([P, 2, S], F32, name="diff%d" % t) for t in range(TILES)]
-        sig = [keep.tile([P, 2, S], F32, name="sig%d" % t) for t in range(TILES)]
+        sig = {}
+        reuse = {(2, 1): "turned0", (3, 0): "turned1"}
         prod = [keep.tile([P, 2, S], F32, name="prod%d" % t) for t in range(TILES)]
         res = [keep.tile([P, S], F32, name="res%d" % t) for t in range(TILES)]
         outv = out.rearrange("(p t) j -> p t j", t=TILES)
+        accs = {}
+
+        def multiply(t, pieces):
+            width = S // pieces
+            for h in range(pieces):
+                cols = slice(h * width, (h + 1) * width)
+                acc = psum.tile([P, width], F32, name="acc%d_%d" % (t, h), tag="acc%d_%d" % (t, h))
+                product(t, acc[:], cols)
+                accs[(t, h)] = acc
 
         def scores(t, pieces):
             width = S // pieces
             for h in range(pieces):
                 cols = slice(h * width, (h + 1) * width)
-                acc = psum.tile([P, width], F32, name="acc%d_%d" % (t, h))
-                product(t, acc[:], cols)
-                nc.scalar.copy(out=windows[t][:, cols], in_=acc[:])
-                nc.scalar.copy(out=own[t][:, cols], in_=acc[:])
+                nc.scalar.copy(out=windows[t][:, cols], in_=accs[(t, h)][:])
+                nc.scalar.copy(out=own[t][:, cols], in_=accs[(t, h)][:])
 
-        def gather(t, l, pieces):
+        def gather(t, l, pieces, spieces=1):
             width = S // pieces
+            sig[(t, l)] = keep.tile([P, S], F32, name="sig%d_%d" % (t, l), tag=reuse.get((t, l), "sig%d_%d" % (t, l)))
             for h in range(pieces):
                 cols = slice(h * width, (h + 1) * width)
                 o = lists[l][:, h * width // 16 : (h + 1) * width // 16]
                 nc.vector.tensor_tensor(out=diff[t][:, l, cols], in0=windows[t][:].indirect(o), in1=own[t][:, cols], op=ALU.subtract)
-            nc.scalar.activation(out=sig[t][:, l, :], in_=diff[t][:, l, :], func=ACT.Sigmoid)
+                if spieces > 1:
+                    nc.scalar.activation(out=sig[(t, l)][:, cols], in_=diff[t][:, l, cols], func=ACT.Sigmoid)
+            if spieces == 1:
+                nc.scalar.activation(out=sig[(t, l)][:], in_=diff[t][:, l, :], func=ACT.Sigmoid)
 
-        def weigh(t, l):
-            nc.vector.tensor_tensor(out=prod[t][:, l, :], in0=sig[t][:, l, :], in1=gains[l][t // 2][:, t % 2, :], op=ALU.mult)
+        def weigh(t, l, cols=slice(0, S)):
+            nc.vector.tensor_tensor(out=prod[t][:, l, cols], in0=sig[(t, l)][:, cols], in1=gains[l][t // 2][:, t % 2, cols], op=ALU.mult)
 
-        def finish(t):
-            nc.vector.tensor_tensor(out=res[t][:], in0=prod[t][:, 0, :], in1=prod[t][:, 1, :], op=ALU.add)
+        def finish(t, cols=slice(0, S)):
+            nc.vector.tensor_tensor(out=res[t][:, cols], in0=prod[t][:, 0, cols], in1=prod[t][:, 1, cols], op=ALU.add)
+            nc.sync.dma_start(out=outv[:, t, cols], in_=res[t][:, cols])
+
+        def finish_pe(t):
+            summed = psum.tile([P, S], F32, name="summed%d" % t, tag="acc0_%d" % t)
+            turned = keep.tile([P, S], F32, name="turned%d" % t, tag="turned%d" % t)
+            for b in range(4):
+                blk = slice(b * P, (b + 1) * P)
+                for l in range(2):
+                    nc.tensor.matmul(out=summed[:, blk], lhsT=prod[t][:, l, blk], rhs=ident[:], start=(l == 0), stop=(l == 1), is_transpose=True)
+            nc.scalar.copy(out=turned[:], in_=summed[:])
+            back = psum.tile([P, S], F32, name="back%d" % t)
+            for b in range(4):
+                blk = slice(b * P, (b + 1) * P)
+                nc.tensor.transpose(back[:, blk], turned[:, blk], ident[:])
+            nc.scalar.copy(out=res[t][:], in_=back[:])
             nc.sync.dma_start(out=outv[:, t, :], in_=res[t][:])
 
-        scores(0, 2)
+        multiply(0, 2)
+        for t in range(1, TILES):
+            multiply(t, 1)
+        nc.scalar.copy(out=windows[0][:, :HALF], in_=accs[(0, 0)][:])
+        nc.vector.tensor_copy(out=own[0][:, :HALF], in_=accs[(0, 0)][:])
+        nc.scalar.copy(out=windows[0][:, HALF:S], in_=accs[(0, 1)][:])
+        nc.scalar.copy(out=own[0][:, HALF:], in_=accs[(0, 1)][:])
         scores(1, 1)
         gather(0, 0, 2)
         gather(0, 1, 1)
+        gather(1, 0, 1)
+        weigh(0, 0)
+        weigh(0, 1)
+        gather(1, 1, 1)
         scores(2, 1)
         scores(3, 1)
-        for t in range(1, TILES):
-            gather(t, 0, 1)
-            weigh(t - 1, 0)
-            gather(t, 1, 1)
-            weigh(t - 1, 1)
-            if t > 1:
-                finish(t - 2)
-        weigh(TILES - 1, 0)
-        finish(TILES - 2)
-        weigh(TILES - 1, 1)
-        finish(TILES - 1)
+        finish_pe(0)
+        gather(2, 0, 1)
+        weigh(1, 0)
+        weigh(1, 1)
+        finish_pe(1)
+        gather(2, 1, 1)
+        gather(3, 0, 1)
+        weigh(2, 0)
+        weigh(2, 1)
+        gather(3, 1, 1)
+        finish(2)
+        weigh(3, 0)
+        weigh(3, 1, slice(0, HALF))
+        weigh(3, 1, slice(HALF, S))
+        finish(3, slice(0, HALF))
+        finish(3, slice(HALF, S))

@@ -44,10 +44,10 @@ def tile_picked_lamrank_none_p_kernel(tc, x_words, x_scales, w1, dg1, dg2, offs,
         nc.scalar.activation(out=warm2[:], in_=warm[:], func=ACT.Sigmoid)
         make_identity(nc, ident[:])
 
-        nc.sync.dma_start(out=offs_sb[:], in_=offs)
         nc.sync.dma_start(out=w_raw[:], in_=w1.rearrange("(p j) m -> p j m", j=4))
-        for q in range(4):
-            nc.sync.dma_start(out=xs_all[32 * q : 32 * q + 4, :].bitcast(I32), in_=x_scales[0, 4 * q : 4 * q + 4, :].bitcast(I32))
+        for r in range(4):
+            nc.sync.dma_start(out=xs_all[r:P:32, :].bitcast(I32), in_=x_scales[0, r:16:4, :].bitcast(I32))
+        nc.sync.dma_start(out=offs_sb[:], in_=offs)
         nc.sync.dma_start(out=xw_all[:], in_=x_words[0].rearrange("p n t -> p (n t)").bitcast(I32))
         nc.sync.dma_start(out=p1_sb[:], in_=p1)
         nc.sync.dma_start(out=p2_sb[:], in_=p2)
@@ -62,8 +62,8 @@ def tile_picked_lamrank_none_p_kernel(tc, x_words, x_scales, w1, dg1, dg2, offs,
         w_codes = {}
         w_scales = [keep.tile([P, 2 * P], U8, name="w_scales%d" % h, align_bytes=64) for h in range(2)]
         src = w_raw[:].rearrange("p j (m t) -> p m j t", t=TILES)
-        for h in range(2):
-            nc.scalar.copy(out=w_grp[h][:].rearrange("p t m j -> p m j t"), in_=src[:, :, :, 2 * h : 2 * h + 2])
+        nc.vector.tensor_copy(out=w_grp[0][:].rearrange("p t m j -> p m j t"), in_=src[:, :, :, 0:2])
+        nc.scalar.copy(out=w_grp[1][:].rearrange("p t m j -> p m j t"), in_=src[:, :, :, 2:4])
 
         xs = keep.tile([P, S], U8, name="xs", align_bytes=64)
         xw = keep.tile([P, S], U32, name="xw", align_bytes=64)
@@ -72,113 +72,118 @@ def tile_picked_lamrank_none_p_kernel(tc, x_words, x_scales, w1, dg1, dg2, offs,
             w_codes[h] = keep.tile([P, 2 * P], U32, name="w_codes%d" % h, tag=tag, align_bytes=64)
             nc.vector.quantize_mx(out=w_codes[h][:].bitcast(FP8X4), scales=w_scales[h][:], in_=w_grp[h][:].rearrange("p t m j -> p (t m j)"))
 
-        def pick(h):
-            nc.vector.tensor_copy(out=xw[:, h * HALF : (h + 1) * HALF], in_=xw_all[:].bitcast(U32).indirect(offs_sb[:, 16 * h : 16 * h + 16]))
-
         nc.vector.tensor_copy(out=xs[:], in_=xs_all[:].indirect(offs_sb[:]))
         quantize(0, "early")
-        pick(0)
-        pick(1)
+        for h in range(2):
+            nc.vector.tensor_copy(out=xw[:, h * HALF : (h + 1) * HALF], in_=xw_all[:].bitcast(U32).indirect(offs_sb[:, 16 * h : 16 * h + 16]))
         quantize(1, "late")
 
-        def product(t, acc, cols):
+        def multiply(t, c0, c1, tag):
+            acc = psum.tile([P, c1 - c0], F32, name="acc_" + tag, tag=tag)
             nc.tensor.matmul_mx(
-                out=acc,
+                out=acc[:],
                 lhsT=w_codes[t // 2][:, t % 2 * P : (t % 2 + 1) * P].bitcast(FP8X4),
                 lhsT_scale=w_scales[t // 2][:, t % 2 * P : (t % 2 + 1) * P],
-                rhs=xw[:, cols].bitcast(FP8X4),
-                rhs_scale=xs[:, cols],
+                rhs=xw[:, c0:c1].bitcast(FP8X4),
+                rhs_scale=xs[:, c0:c1],
                 start=True,
                 stop=True,
             )
+            return acc
 
         own = [keep.tile([P, S], F32, name="own%d" % t) for t in range(TILES)]
-        diff = [keep.tile([P, 2, S], F32, name="diff%d" % t) for t in range(TILES)]
-        sig = {}
-        reuse = {(2, 1): "turned0", (3, 0): "turned1"}
-        prod = [keep.tile([P, 2, S], F32, name="prod%d" % t) for t in range(TILES)]
         res = [keep.tile([P, S], F32, name="res%d" % t) for t in range(TILES)]
         outv = out.rearrange("(p t) j -> p t j", t=TILES)
-        accs = {}
+        made = {}
+        reuse = {"sig21": "turned00", "sig30": "turned10"}
 
-        def multiply(t, pieces):
-            width = S // pieces
-            for h in range(pieces):
-                cols = slice(h * width, (h + 1) * width)
-                acc = psum.tile([P, width], F32, name="acc%d_%d" % (t, h), tag="acc%d_%d" % (t, h))
-                product(t, acc[:], cols)
-                accs[(t, h)] = acc
+        def fresh(kind, t, l):
+            name = "%s%d%d" % (kind, t, l)
+            made[name] = keep.tile([P, S], F32, name=name, tag=reuse.get(name, name))
+            return made[name]
 
-        def scores(t, pieces):
-            width = S // pieces
-            for h in range(pieces):
-                cols = slice(h * width, (h + 1) * width)
-                nc.scalar.copy(out=windows[t][:, cols], in_=accs[(t, h)][:])
-                nc.scalar.copy(out=own[t][:, cols], in_=accs[(t, h)][:])
+        def scores(t, acc):
+            nc.scalar.copy(out=windows[t][:, :S], in_=acc[:])
+            nc.scalar.copy(out=own[t][:], in_=acc[:])
 
-        def gather(t, l, pieces, spieces=1):
+        def gather(t, l, pieces=1):
+            diff = fresh("diff", t, l)
             width = S // pieces
-            sig[(t, l)] = keep.tile([P, S], F32, name="sig%d_%d" % (t, l), tag=reuse.get((t, l), "sig%d_%d" % (t, l)))
             for h in range(pieces):
                 cols = slice(h * width, (h + 1) * width)
                 o = lists[l][:, h * width // 16 : (h + 1) * width // 16]
-                nc.vector.tensor_tensor(out=diff[t][:, l, cols], in0=windows[t][:].indirect(o), in1=own[t][:, cols], op=ALU.subtract)
-                if spieces > 1:
-                    nc.scalar.activation(out=sig[(t, l)][:, cols], in_=diff[t][:, l, cols], func=ACT.Sigmoid)
-            if spieces == 1:
-                nc.scalar.activation(out=sig[(t, l)][:], in_=diff[t][:, l, :], func=ACT.Sigmoid)
+                nc.vector.tensor_tensor(out=diff[:, cols], in0=windows[t][:].indirect(o), in1=own[t][:, cols], op=ALU.subtract)
 
-        def weigh(t, l, cols=slice(0, S)):
-            nc.vector.tensor_tensor(out=prod[t][:, l, cols], in0=sig[(t, l)][:, cols], in1=gains[l][t // 2][:, t % 2, cols], op=ALU.mult)
+        def squash(t, l):
+            nc.scalar.activation(out=fresh("sig", t, l)[:], in_=made["diff%d%d" % (t, l)][:], func=ACT.Sigmoid)
 
-        def finish(t, cols=slice(0, S)):
-            nc.vector.tensor_tensor(out=res[t][:, cols], in0=prod[t][:, 0, cols], in1=prod[t][:, 1, cols], op=ALU.add)
-            nc.sync.dma_start(out=outv[:, t, cols], in_=res[t][:, cols])
+        def weigh(t, l, pieces=1):
+            prod = fresh("prod", t, l)
+            width = S // pieces
+            for h in range(pieces):
+                cols = slice(h * width, (h + 1) * width)
+                nc.vector.tensor_tensor(out=prod[:, cols], in0=made["sig%d%d" % (t, l)][:, cols], in1=gains[l][t // 2][:, t % 2, cols], op=ALU.mult)
 
-        def finish_pe(t):
-            summed = psum.tile([P, S], F32, name="summed%d" % t, tag="acc0_%d" % t)
-            turned = keep.tile([P, S], F32, name="turned%d" % t, tag="turned%d" % t)
+        def finish(t, pieces=1):
+            width = S // pieces
+            for h in range(pieces):
+                cols = slice(h * width, (h + 1) * width)
+                nc.vector.tensor_tensor(out=res[t][:, cols], in0=made["prod%d0" % t][:, cols], in1=made["prod%d1" % t][:, cols], op=ALU.add)
+                nc.sync.dma_start(out=outv[:, t, cols], in_=res[t][:, cols])
+
+        def sum_turned(t, tag):
+            summed = psum.tile([P, S], F32, name="summed%d" % t, tag=tag)
             for b in range(4):
                 blk = slice(b * P, (b + 1) * P)
                 for l in range(2):
-                    nc.tensor.matmul(out=summed[:, blk], lhsT=prod[t][:, l, blk], rhs=ident[:], start=(l == 0), stop=(l == 1), is_transpose=True)
-            nc.scalar.copy(out=turned[:], in_=summed[:])
-            back = psum.tile([P, S], F32, name="back%d" % t)
+                    nc.tensor.matmul(out=summed[:, blk], lhsT=made["prod%d%d" % (t, l)][:, blk], rhs=ident[:], start=(l == 0), stop=(l == 1), is_transpose=True)
+            nc.scalar.copy(out=fresh("turned", t, 0)[:], in_=summed[:])
+
+        def turn_back(t, tag):
+            back = psum.tile([P, S], F32, name="back%d" % t, tag=tag)
             for b in range(4):
                 blk = slice(b * P, (b + 1) * P)
-                nc.tensor.transpose(back[:, blk], turned[:, blk], ident[:])
+                nc.tensor.transpose(back[:, blk], made["turned%d0" % t][:, blk], ident[:])
             nc.scalar.copy(out=res[t][:], in_=back[:])
             nc.sync.dma_start(out=outv[:, t, :], in_=res[t][:])
 
-        multiply(0, 2)
-        for t in range(1, TILES):
-            multiply(t, 1)
-        nc.scalar.copy(out=windows[0][:, :HALF], in_=accs[(0, 0)][:])
-        nc.vector.tensor_copy(out=own[0][:, :HALF], in_=accs[(0, 0)][:])
-        nc.scalar.copy(out=windows[0][:, HALF:S], in_=accs[(0, 1)][:])
-        nc.scalar.copy(out=own[0][:, HALF:], in_=accs[(0, 1)][:])
-        scores(1, 1)
+        a0 = multiply(0, 0, HALF, "b0")
+        a1 = multiply(0, HALF, S, "b1")
+        accs = [None] + [multiply(t, 0, S, "b%d" % (2 + t)) for t in range(1, TILES)]
+        nc.scalar.copy(out=windows[0][:, :HALF], in_=a0[:])
+        nc.vector.tensor_copy(out=own[0][:, :HALF], in_=a0[:])
+        nc.scalar.copy(out=windows[0][:, HALF:S], in_=a1[:])
+        nc.scalar.copy(out=own[0][:, HALF:], in_=a1[:])
+        scores(1, accs[1])
         gather(0, 0, 2)
-        gather(0, 1, 1)
-        gather(1, 0, 1)
+        squash(0, 0)
+        gather(0, 1)
+        squash(0, 1)
+        gather(1, 0)
+        squash(1, 0)
         weigh(0, 0)
         weigh(0, 1)
-        gather(1, 1, 1)
-        scores(2, 1)
-        scores(3, 1)
-        finish_pe(0)
-        gather(2, 0, 1)
+        gather(1, 1)
+        squash(1, 1)
+        scores(2, accs[2])
+        scores(3, accs[3])
+        sum_turned(0, "b0")
+        turn_back(0, "b6")
+        gather(2, 0)
+        squash(2, 0)
         weigh(1, 0)
         weigh(1, 1)
-        finish_pe(1)
-        gather(2, 1, 1)
-        gather(3, 0, 1)
+        sum_turned(1, "b1")
+        turn_back(1, "b7")
+        gather(2, 1)
+        squash(2, 1)
+        gather(3, 0)
+        squash(3, 0)
         weigh(2, 0)
         weigh(2, 1)
-        gather(3, 1, 1)
+        gather(3, 1)
+        squash(3, 1)
         finish(2)
         weigh(3, 0)
-        weigh(3, 1, slice(0, HALF))
-        weigh(3, 1, slice(HALF, S))
-        finish(3, slice(0, HALF))
-        finish(3, slice(HALF, S))
+        weigh(3, 1, 2)
+        finish(3, 2)

@@ -14,8 +14,11 @@ ALU = mybir.AluOpType
 ACT = mybir.ActivationFunctionType
 
 P = 128
+PACK = 4
+STRIPE = 16
 K, T, S, N = 512, 2048, 512, 512
 TILES = N // P
+PAIR = 2
 HALF = S // 2
 FLOPS = 2 * K * N * S
 
@@ -26,164 +29,146 @@ def tile_picked_lamrank_none_p_kernel(tc, x_words, x_scales, w1, dg1, dg2, offs,
         keep = ctx.enter_context(tc.tile_pool(name="keep", bufs=1))
         psum = ctx.enter_context(tc.psum_pool(name="psum", bufs=1))
 
-        offs_sb = keep.tile([P, S // 16], U16, name="offs_sb")
-        p1_sb = keep.tile([P, S // 16], U16, name="p1_sb")
-        p2_sb = keep.tile([P, S // 16], U16, name="p2_sb")
-        lists = [p1_sb, p2_sb]
-        w_raw = keep.tile([P, 4, N], F32, name="w_raw")
-        xs_all = keep.tile([P, T], U8, name="xs_all", tag="early", align_bytes=64)
-        xw_all = keep.tile([P, T], I32, name="xw_all", tag="late", align_bytes=64)
-        warm = keep.tile([P, 8], F32, name="warm")
-        warm2 = keep.tile([P, 8], F32, name="warm2")
+        offs_sb = keep.tile([P, S // STRIPE], U16, name="offs_sb")
+        p1_sb = keep.tile([P, S // STRIPE], U16, name="p1_sb")
+        p2_sb = keep.tile([P, S // STRIPE], U16, name="p2_sb")
+        partners = [p1_sb, p2_sb]
+        w_raw = keep.tile([P, PACK, N], F32, name="w_raw")
+        scale_table = keep.tile([P, T], U8, name="scale_table", tag="scale_table", align_bytes=64)
+        word_table = keep.tile([P, T], I32, name="word_table", tag="word_table", align_bytes=64)
         ident = keep.tile([P, P], F32, name="ident")
-        windows = [keep.tile([P, 2 * S], F32, name="win%d" % t) for t in range(TILES)]
-        gains = [[keep.tile([P, 2, S], F32, name="gain%d_%d" % (l, h)) for h in range(2)] for l in range(2)]
+        windows = [keep.tile([P, 2 * S], F32, name="window%d" % t) for t in range(TILES)]
+        gains = [[keep.tile([P, PAIR, S], F32, name="gain%d_%d" % (side, h)) for h in range(TILES // PAIR)] for side in range(2)]
 
-        nc.vector.memset(xs_all[:].bitcast(I32), 0)
-        nc.vector.memset(warm[:], 0.0)
-        nc.scalar.activation(out=warm2[:], in_=warm[:], func=ACT.Sigmoid)
+        nc.vector.memset(scale_table[:].bitcast(I32), 0)
         make_identity(nc, ident[:])
 
-        nc.sync.dma_start(out=w_raw[:], in_=w1.rearrange("(p j) m -> p j m", j=4))
+        nc.sync.dma_start(out=w_raw[:], in_=w1.rearrange("(p j) m -> p j m", j=PACK))
         for r in range(4):
-            nc.sync.dma_start(out=xs_all[r:P:32, :].bitcast(I32), in_=x_scales[0, r:16:4, :].bitcast(I32))
+            nc.sync.dma_start(out=scale_table[r:P:32, :].bitcast(I32), in_=x_scales[0, r:16:4, :].bitcast(I32))
         nc.sync.dma_start(out=offs_sb[:], in_=offs)
-        nc.sync.dma_start(out=xw_all[:], in_=x_words[0].rearrange("p n t -> p (n t)").bitcast(I32))
+        nc.sync.dma_start(out=word_table[:], in_=x_words[0].rearrange("p n t -> p (n t)").bitcast(I32))
         nc.sync.dma_start(out=p1_sb[:], in_=p1)
         nc.sync.dma_start(out=p2_sb[:], in_=p2)
-        dgv = [dg1.rearrange("(p t) j -> p t j", t=TILES), dg2.rearrange("(p t) j -> p t j", t=TILES)]
-        for h in range(2):
-            for l in range(2):
-                nc.sync.dma_start(out=gains[l][h][:], in_=dgv[l][:, 2 * h : 2 * h + 2, :])
+        gain_rows = [dg.rearrange("(p t) j -> p t j", t=TILES) for dg in (dg1, dg2)]
+        for h in range(TILES // PAIR):
+            for side in range(2):
+                nc.sync.dma_start(out=gains[side][h][:], in_=gain_rows[side][:, PAIR * h : PAIR * (h + 1), :])
         for t in range(TILES):
             nc.vector.memset(windows[t][:, S:], 0.0)
 
-        w_grp = [keep.tile([P, 2, P, 4], BF16, name="w_grp%d" % h, align_bytes=64) for h in range(2)]
-        w_codes = {}
-        w_scales = [keep.tile([P, 2 * P], U8, name="w_scales%d" % h, align_bytes=64) for h in range(2)]
-        src = w_raw[:].rearrange("p j (m t) -> p m j t", t=TILES)
-        nc.vector.tensor_copy(out=w_grp[0][:].rearrange("p t m j -> p m j t"), in_=src[:, :, :, 0:2])
-        nc.scalar.copy(out=w_grp[1][:].rearrange("p t m j -> p m j t"), in_=src[:, :, :, 2:4])
+        w_grouped = [keep.tile([P, PAIR, P, PACK], BF16, name="w_grouped%d" % h, align_bytes=64) for h in range(TILES // PAIR)]
+        w_scales = [keep.tile([P, PAIR * P], U8, name="w_scales%d" % h, align_bytes=64) for h in range(TILES // PAIR)]
+        dealt = w_raw[:].rearrange("p j (c t) -> p c j t", t=TILES)
+        nc.vector.tensor_copy(out=w_grouped[0][:].rearrange("p t c j -> p c j t"), in_=dealt[:, :, :, :PAIR])
+        nc.scalar.copy(out=w_grouped[1][:].rearrange("p t c j -> p c j t"), in_=dealt[:, :, :, PAIR:])
 
-        xs = keep.tile([P, S], U8, name="xs", align_bytes=64)
-        xw = keep.tile([P, S], U32, name="xw", align_bytes=64)
+        x_bytes = keep.tile([P, S], U8, name="x_bytes", align_bytes=64)
+        x_codes = keep.tile([P, S], U32, name="x_codes", align_bytes=64)
 
         def quantize(h, tag):
-            w_codes[h] = keep.tile([P, 2 * P], U32, name="w_codes%d" % h, tag=tag, align_bytes=64)
-            nc.vector.quantize_mx(out=w_codes[h][:].bitcast(FP8X4), scales=w_scales[h][:], in_=w_grp[h][:].rearrange("p t m j -> p (t m j)"))
+            codes = keep.tile([P, PAIR * P], U32, name="w_codes%d" % h, tag=tag, align_bytes=64)
+            nc.vector.quantize_mx(out=codes[:].bitcast(FP8X4), scales=w_scales[h][:], in_=w_grouped[h][:].rearrange("p t c j -> p (t c j)"))
+            return codes
 
-        nc.vector.tensor_copy(out=xs[:], in_=xs_all[:].indirect(offs_sb[:]))
-        quantize(0, "early")
-        for h in range(2):
-            nc.vector.tensor_copy(out=xw[:, h * HALF : (h + 1) * HALF], in_=xw_all[:].bitcast(U32).indirect(offs_sb[:, 16 * h : 16 * h + 16]))
-        quantize(1, "late")
+        def halves():
+            return [slice(0, HALF), slice(HALF, S)]
 
-        def multiply(t, c0, c1, tag):
-            acc = psum.tile([P, c1 - c0], F32, name="acc_" + tag, tag=tag)
+        def entries(list_tile, cols):
+            return list_tile[:, cols.start // STRIPE : cols.stop // STRIPE]
+
+        nc.vector.tensor_copy(out=x_bytes[:], in_=scale_table[:].indirect(offs_sb[:]))
+        w_codes = [quantize(0, "scale_table")]
+        for cols in halves():
+            nc.vector.tensor_copy(out=x_codes[:, cols], in_=word_table[:].bitcast(U32).indirect(entries(offs_sb, cols)))
+        w_codes.append(quantize(1, "word_table"))
+
+        def multiply(t, cols, bank):
+            acc = psum.tile([P, cols.stop - cols.start], F32, name="acc_" + bank, tag=bank)
+            rankers = slice(t % PAIR * P, (t % PAIR + 1) * P)
             nc.tensor.matmul_mx(
                 out=acc[:],
-                lhsT=w_codes[t // 2][:, t % 2 * P : (t % 2 + 1) * P].bitcast(FP8X4),
-                lhsT_scale=w_scales[t // 2][:, t % 2 * P : (t % 2 + 1) * P],
-                rhs=xw[:, c0:c1].bitcast(FP8X4),
-                rhs_scale=xs[:, c0:c1],
+                lhsT=w_codes[t // PAIR][:, rankers].bitcast(FP8X4),
+                lhsT_scale=w_scales[t // PAIR][:, rankers],
+                rhs=x_codes[:, cols].bitcast(FP8X4),
+                rhs_scale=x_bytes[:, cols],
                 start=True,
                 stop=True,
             )
             return acc
 
         own = [keep.tile([P, S], F32, name="own%d" % t) for t in range(TILES)]
-        res = [keep.tile([P, S], F32, name="res%d" % t) for t in range(TILES)]
-        outv = out.rearrange("(p t) j -> p t j", t=TILES)
-        made = {}
-        reuse = {"sig21": "turned00", "sig30": "turned10"}
+        result = [keep.tile([P, S], F32, name="result%d" % t) for t in range(TILES)]
+        out_rows = out.rearrange("(p t) j -> p t j", t=TILES)
+        whole = [slice(0, S)]
+        blocks = [slice(b * P, (b + 1) * P) for b in range(S // P)]
+        sigmoids = {}
+        products = {}
 
-        def fresh(kind, t, l):
-            name = "%s%d%d" % (kind, t, l)
-            made[name] = keep.tile([P, S], F32, name=name, tag=reuse.get(name, name))
-            return made[name]
-
-        def scores(t, acc):
+        def copy_scores(t, acc):
             nc.scalar.copy(out=windows[t][:, :S], in_=acc[:])
             nc.scalar.copy(out=own[t][:], in_=acc[:])
 
-        def gather(t, l, pieces=1):
-            diff = fresh("diff", t, l)
-            width = S // pieces
-            for h in range(pieces):
-                cols = slice(h * width, (h + 1) * width)
-                o = lists[l][:, h * width // 16 : (h + 1) * width // 16]
-                nc.vector.tensor_tensor(out=diff[:, cols], in0=windows[t][:].indirect(o), in1=own[t][:, cols], op=ALU.subtract)
+        def compare(t, side, pieces=whole, tag=None):
+            name = "%d_%d" % (t, side)
+            diff = keep.tile([P, S], F32, name="diff" + name)
+            for cols in pieces:
+                nc.vector.tensor_tensor(out=diff[:, cols], in0=windows[t][:].indirect(entries(partners[side], cols)), in1=own[t][:, cols], op=ALU.subtract)
+            sigmoids[(t, side)] = keep.tile([P, S], F32, name="sigmoid" + name, tag=tag or "sigmoid" + name)
+            nc.scalar.activation(out=sigmoids[(t, side)][:], in_=diff[:], func=ACT.Sigmoid)
 
-        def squash(t, l):
-            nc.scalar.activation(out=fresh("sig", t, l)[:], in_=made["diff%d%d" % (t, l)][:], func=ACT.Sigmoid)
+        def weigh(t, side, pieces=whole):
+            products[(t, side)] = keep.tile([P, S], F32, name="product%d_%d" % (t, side))
+            for cols in pieces:
+                nc.vector.tensor_tensor(out=products[(t, side)][:, cols], in0=sigmoids[(t, side)][:, cols], in1=gains[side][t // PAIR][:, t % PAIR, cols], op=ALU.mult)
 
-        def weigh(t, l, pieces=1):
-            prod = fresh("prod", t, l)
-            width = S // pieces
-            for h in range(pieces):
-                cols = slice(h * width, (h + 1) * width)
-                nc.vector.tensor_tensor(out=prod[:, cols], in0=made["sig%d%d" % (t, l)][:, cols], in1=gains[l][t // 2][:, t % 2, cols], op=ALU.mult)
+        def add_on_vector(t, pieces=whole):
+            for cols in pieces:
+                nc.vector.tensor_tensor(out=result[t][:, cols], in0=products[(t, 0)][:, cols], in1=products[(t, 1)][:, cols], op=ALU.add)
+                nc.sync.dma_start(out=out_rows[:, t, cols], in_=result[t][:, cols])
 
-        def finish(t, pieces=1):
-            width = S // pieces
-            for h in range(pieces):
-                cols = slice(h * width, (h + 1) * width)
-                nc.vector.tensor_tensor(out=res[t][:, cols], in0=made["prod%d0" % t][:, cols], in1=made["prod%d1" % t][:, cols], op=ALU.add)
-                nc.sync.dma_start(out=outv[:, t, cols], in_=res[t][:, cols])
+        def add_on_tensor(t, bank):
+            summed = psum.tile([P, S], F32, name="summed%d" % t, tag=bank)
+            for blk in blocks:
+                for side in range(2):
+                    nc.tensor.matmul(out=summed[:, blk], lhsT=products[(t, side)][:, blk], rhs=ident[:], start=(side == 0), stop=(side == 1), is_transpose=True)
+            turned = keep.tile([P, S], F32, name="turned%d" % t, tag="turned%d" % t)
+            nc.scalar.copy(out=turned[:], in_=summed[:])
+            back = psum.tile([P, S], F32, name="back%d" % t)
+            for blk in blocks:
+                nc.tensor.transpose(back[:, blk], turned[:, blk], ident[:])
+            nc.scalar.copy(out=result[t][:], in_=back[:])
+            nc.sync.dma_start(out=out_rows[:, t, :], in_=result[t][:])
 
-        def sum_turned(t, tag):
-            summed = psum.tile([P, S], F32, name="summed%d" % t, tag=tag)
-            for b in range(4):
-                blk = slice(b * P, (b + 1) * P)
-                for l in range(2):
-                    nc.tensor.matmul(out=summed[:, blk], lhsT=made["prod%d%d" % (t, l)][:, blk], rhs=ident[:], start=(l == 0), stop=(l == 1), is_transpose=True)
-            nc.scalar.copy(out=fresh("turned", t, 0)[:], in_=summed[:])
+        low, high = halves()
+        acc_low = multiply(0, low, "bank_low")
+        acc_high = multiply(0, high, "bank_high")
+        accs = {t: multiply(t, whole[0], "bank%d" % t) for t in range(1, TILES)}
+        nc.scalar.copy(out=windows[0][:, low], in_=acc_low[:])
+        nc.vector.tensor_copy(out=own[0][:, low], in_=acc_low[:])
+        nc.scalar.copy(out=windows[0][:, high], in_=acc_high[:])
+        nc.scalar.copy(out=own[0][:, high], in_=acc_high[:])
+        copy_scores(1, accs[1])
 
-        def turn_back(t, tag):
-            back = psum.tile([P, S], F32, name="back%d" % t, tag=tag)
-            for b in range(4):
-                blk = slice(b * P, (b + 1) * P)
-                nc.tensor.transpose(back[:, blk], made["turned%d0" % t][:, blk], ident[:])
-            nc.scalar.copy(out=res[t][:], in_=back[:])
-            nc.sync.dma_start(out=outv[:, t, :], in_=res[t][:])
-
-        a0 = multiply(0, 0, HALF, "b0")
-        a1 = multiply(0, HALF, S, "b1")
-        accs = [None] + [multiply(t, 0, S, "b%d" % (2 + t)) for t in range(1, TILES)]
-        nc.scalar.copy(out=windows[0][:, :HALF], in_=a0[:])
-        nc.vector.tensor_copy(out=own[0][:, :HALF], in_=a0[:])
-        nc.scalar.copy(out=windows[0][:, HALF:S], in_=a1[:])
-        nc.scalar.copy(out=own[0][:, HALF:], in_=a1[:])
-        scores(1, accs[1])
-        gather(0, 0, 2)
-        squash(0, 0)
-        gather(0, 1)
-        squash(0, 1)
-        gather(1, 0)
-        squash(1, 0)
+        compare(0, 0, halves())
+        compare(0, 1)
+        compare(1, 0)
         weigh(0, 0)
         weigh(0, 1)
-        gather(1, 1)
-        squash(1, 1)
-        scores(2, accs[2])
-        scores(3, accs[3])
-        sum_turned(0, "b0")
-        turn_back(0, "b6")
-        gather(2, 0)
-        squash(2, 0)
+        compare(1, 1)
+        copy_scores(2, accs[2])
+        copy_scores(3, accs[3])
+        add_on_tensor(0, "bank_low")
+        compare(2, 0)
         weigh(1, 0)
         weigh(1, 1)
-        sum_turned(1, "b1")
-        turn_back(1, "b7")
-        gather(2, 1)
-        squash(2, 1)
-        gather(3, 0)
-        squash(3, 0)
+        add_on_tensor(1, "bank_high")
+        compare(2, 1, tag="turned0")
+        compare(3, 0, tag="turned1")
         weigh(2, 0)
         weigh(2, 1)
-        gather(3, 1)
-        squash(3, 1)
-        finish(2)
+        compare(3, 1)
+        add_on_vector(2)
         weigh(3, 0)
-        weigh(3, 1, 2)
-        finish(3, 2)
+        weigh(3, 1, halves())
+        add_on_vector(3, halves())

@@ -19,6 +19,7 @@ STRIPE = 16
 K, T, S, N = 512, 2048, 512, 512
 TILES = N // P
 PAIR = 2
+SIDES = 2
 HALF = S // 2
 FLOPS = 2 * K * N * S
 
@@ -37,11 +38,13 @@ def tile_picked_lamrank_none_p_kernel(tc, x_words, x_scales, w1, dg1, dg2, offs,
         scale_table = keep.tile([P, T], U8, name="scale_table", tag="scale_table", align_bytes=64)
         word_table = keep.tile([P, T], I32, name="word_table", tag="word_table", align_bytes=64)
         ident = keep.tile([P, P], F32, name="ident")
-        windows = [keep.tile([P, 2 * S], F32, name="window%d" % t) for t in range(TILES)]
-        gains = [[keep.tile([P, PAIR, S], F32, name="gain%d_%d" % (side, h)) for h in range(TILES // PAIR)] for side in range(2)]
+        windows = [keep.tile([P, S], F32, name="window%d" % t) for t in range(TILES)]
+        gains = [keep.tile([P, SIDES, PAIR, S], F32, name="gain%d" % h) for h in range(TILES // PAIR)]
 
         nc.vector.memset(scale_table[:].bitcast(I32), 0)
         make_identity(nc, ident[:])
+        warm = keep.tile([P, 8], F32, name="warm")
+        nc.scalar.activation(out=warm[:, :1], in_=ident[:, :1], func=ACT.Sigmoid)
 
         nc.sync.dma_start(out=w_raw[:], in_=w1.rearrange("(p j) m -> p j m", j=PACK))
         for r in range(4):
@@ -52,16 +55,14 @@ def tile_picked_lamrank_none_p_kernel(tc, x_words, x_scales, w1, dg1, dg2, offs,
         nc.sync.dma_start(out=p2_sb[:], in_=p2)
         gain_rows = [dg.rearrange("(p t) j -> p t j", t=TILES) for dg in (dg1, dg2)]
         for h in range(TILES // PAIR):
-            for side in range(2):
-                nc.sync.dma_start(out=gains[side][h][:], in_=gain_rows[side][:, PAIR * h : PAIR * (h + 1), :])
-        for t in range(TILES):
-            nc.vector.memset(windows[t][:, S:], 0.0)
+            for side in range(SIDES):
+                nc.sync.dma_start(out=gains[h][:, side], in_=gain_rows[side][:, PAIR * h : PAIR * (h + 1), :])
 
         w_grouped = [keep.tile([P, PAIR, P, PACK], BF16, name="w_grouped%d" % h, align_bytes=64) for h in range(TILES // PAIR)]
         w_scales = [keep.tile([P, PAIR * P], U8, name="w_scales%d" % h, align_bytes=64) for h in range(TILES // PAIR)]
         dealt = w_raw[:].rearrange("p j (c t) -> p c j t", t=TILES)
-        nc.vector.tensor_copy(out=w_grouped[0][:].rearrange("p t c j -> p c j t"), in_=dealt[:, :, :, :PAIR])
-        nc.scalar.copy(out=w_grouped[1][:].rearrange("p t c j -> p c j t"), in_=dealt[:, :, :, PAIR:])
+        nc.scalar.copy(out=w_grouped[0][:].rearrange("p t c j -> p c j t"), in_=dealt[:, :, :, :PAIR])
+        nc.vector.tensor_copy(out=w_grouped[1][:].rearrange("p t c j -> p c j t"), in_=dealt[:, :, :, PAIR:])
 
         x_bytes = keep.tile([P, S], U8, name="x_bytes", align_bytes=64)
         x_codes = keep.tile([P, S], U32, name="x_codes", align_bytes=64)
@@ -71,17 +72,16 @@ def tile_picked_lamrank_none_p_kernel(tc, x_words, x_scales, w1, dg1, dg2, offs,
             nc.vector.quantize_mx(out=codes[:].bitcast(FP8X4), scales=w_scales[h][:], in_=w_grouped[h][:].rearrange("p t c j -> p (t c j)"))
             return codes
 
-        def halves():
-            return [slice(0, HALF), slice(HALF, S)]
+        low, high, whole = slice(0, HALF), slice(HALF, S), slice(0, S)
 
         def entries(list_tile, cols):
             return list_tile[:, cols.start // STRIPE : cols.stop // STRIPE]
 
+        late_codes = quantize(1, "w_codes1")
         nc.vector.tensor_copy(out=x_bytes[:], in_=scale_table[:].indirect(offs_sb[:]))
-        w_codes = [quantize(0, "scale_table")]
-        for cols in halves():
+        w_codes = [quantize(0, "scale_table"), late_codes]
+        for cols in (low, high):
             nc.vector.tensor_copy(out=x_codes[:, cols], in_=word_table[:].bitcast(U32).indirect(entries(offs_sb, cols)))
-        w_codes.append(quantize(1, "word_table"))
 
         def multiply(t, cols, bank):
             acc = psum.tile([P, cols.stop - cols.start], F32, name="acc_" + bank, tag=bank)
@@ -97,78 +97,89 @@ def tile_picked_lamrank_none_p_kernel(tc, x_words, x_scales, w1, dg1, dg2, offs,
             )
             return acc
 
-        own = [keep.tile([P, S], F32, name="own%d" % t) for t in range(TILES)]
+        own = [keep.tile([P, HALF], F32, name="own%d" % t) for t in range(TILES)]
+        diff = [keep.tile([P, SIDES, HALF], F32, name="diff%d" % t) for t in range(TILES)]
+        minus = [keep.tile([P, SIDES, HALF], F32, name="minus%d" % t) for t in range(TILES)]
+        product = [keep.tile([P, SIDES, S], F32, name="product%d" % t) for t in range(TILES)]
         result = [keep.tile([P, S], F32, name="result%d" % t) for t in range(TILES)]
         out_rows = out.rearrange("(p t) j -> p t j", t=TILES)
-        whole = [slice(0, S)]
-        blocks = [slice(b * P, (b + 1) * P) for b in range(S // P)]
-        sigmoids = {}
-        products = {}
+        sig_low, sig_high, turned = {}, {}, {}
 
-        def copy_scores(t, acc):
-            nc.scalar.copy(out=windows[t][:, :S], in_=acc[:])
-            nc.scalar.copy(out=own[t][:], in_=acc[:])
+        def gather_low(t):
+            for side in range(SIDES):
+                nc.vector.tensor_tensor(out=diff[t][:, side, :], in0=windows[t][:].indirect(entries(partners[side], low)), in1=own[t][:], op=ALU.subtract)
 
-        def compare(t, side, pieces=whole, tag=None):
-            name = "%d_%d" % (t, side)
-            diff = keep.tile([P, S], F32, name="diff" + name)
+        def gather_high(t, bank):
+            turned[t] = psum.tile([P, S], F32, name="turned%d" % t, tag=bank)
+            for side in range(SIDES):
+                nc.scalar.activation(out=minus[t][:, side, :], in_=windows[t][:].indirect(entries(partners[side], high)), func=ACT.Copy, scale=-1.0)
+                for b in range(HALF // P):
+                    place = turned[t][:, side * HALF + b * P : side * HALF + (b + 1) * P]
+                    nc.tensor.matmul(out=place, lhsT=windows[t][:, HALF + b * P : HALF + (b + 1) * P], rhs=ident[:], start=True, stop=False, is_transpose=True)
+                    nc.tensor.matmul(out=place, lhsT=minus[t][:, side, b * P : (b + 1) * P], rhs=ident[:], start=False, stop=True, is_transpose=True)
+
+        def sigmoid_low(t):
+            sig_low[t] = keep.tile([P, SIDES, HALF], F32, name="sig_low%d" % t)
+            nc.scalar.activation(out=sig_low[t][:], in_=diff[t][:], func=ACT.Sigmoid)
+
+        def sigmoid_high(t, bank):
+            sig_turned = keep.tile([P, S], F32, name="sig_turned%d" % t)
+            nc.scalar.activation(out=sig_turned[:], in_=turned[t][:], func=ACT.Sigmoid, scale=-1.0)
+            sig_high[t] = psum.tile([P, S], F32, name="sig_high%d" % t, tag=bank)
+            for b in range(S // P):
+                nc.tensor.transpose(sig_high[t][:, b * P : (b + 1) * P], sig_turned[:, b * P : (b + 1) * P], ident[:])
+
+        def weigh_low(t):
+            nc.vector.tensor_tensor(out=product[t][:, :, low], in0=sig_low[t][:], in1=gains[t // PAIR][:, :, t % PAIR, low], op=ALU.mult)
+
+        def weigh_high(t):
+            nc.vector.tensor_tensor(out=product[t][:, :, high], in0=sig_high[t][:].rearrange("p (s j) -> p s j", s=SIDES), in1=gains[t // PAIR][:, :, t % PAIR, high], op=ALU.mult)
+
+        def finish(t, pieces=(whole,)):
             for cols in pieces:
-                nc.vector.tensor_tensor(out=diff[:, cols], in0=windows[t][:].indirect(entries(partners[side], cols)), in1=own[t][:, cols], op=ALU.subtract)
-            sigmoids[(t, side)] = keep.tile([P, S], F32, name="sigmoid" + name, tag=tag or "sigmoid" + name)
-            nc.scalar.activation(out=sigmoids[(t, side)][:], in_=diff[:], func=ACT.Sigmoid)
-
-        def weigh(t, side, pieces=whole):
-            products[(t, side)] = keep.tile([P, S], F32, name="product%d_%d" % (t, side))
-            for cols in pieces:
-                nc.vector.tensor_tensor(out=products[(t, side)][:, cols], in0=sigmoids[(t, side)][:, cols], in1=gains[side][t // PAIR][:, t % PAIR, cols], op=ALU.mult)
-
-        def add_on_vector(t, pieces=whole):
-            for cols in pieces:
-                nc.vector.tensor_tensor(out=result[t][:, cols], in0=products[(t, 0)][:, cols], in1=products[(t, 1)][:, cols], op=ALU.add)
+                nc.vector.tensor_tensor(out=result[t][:, cols], in0=product[t][:, 0, cols], in1=product[t][:, 1, cols], op=ALU.add)
                 nc.sync.dma_start(out=out_rows[:, t, cols], in_=result[t][:, cols])
 
-        def add_on_tensor(t, bank):
-            summed = psum.tile([P, S], F32, name="summed%d" % t, tag=bank)
-            for blk in blocks:
-                for side in range(2):
-                    nc.tensor.matmul(out=summed[:, blk], lhsT=products[(t, side)][:, blk], rhs=ident[:], start=(side == 0), stop=(side == 1), is_transpose=True)
-            turned = keep.tile([P, S], F32, name="turned%d" % t, tag="turned%d" % t)
-            nc.scalar.copy(out=turned[:], in_=summed[:])
-            back = psum.tile([P, S], F32, name="back%d" % t)
-            for blk in blocks:
-                nc.tensor.transpose(back[:, blk], turned[:, blk], ident[:])
-            nc.scalar.copy(out=result[t][:], in_=back[:])
-            nc.sync.dma_start(out=out_rows[:, t, :], in_=result[t][:])
+        acc_low = [multiply(t, low, "bank%d" % t) for t in range(PAIR)]
+        acc_high = [multiply(t, high, "bank%d" % (PAIR + t)) for t in range(PAIR)]
+        accs = {t: multiply(t, whole, "bank%d" % (PAIR + t)) for t in range(PAIR, TILES)}
+        for t in range(PAIR):
+            nc.scalar.copy(out=windows[t][:, low], in_=acc_low[t][:])
+            nc.vector.tensor_copy(out=own[t][:], in_=acc_low[t][:])
+        for t in range(PAIR):
+            nc.scalar.copy(out=windows[t][:, high], in_=acc_high[t][:])
 
-        low, high = halves()
-        acc_low = multiply(0, low, "bank_low")
-        acc_high = multiply(0, high, "bank_high")
-        accs = {t: multiply(t, whole[0], "bank%d" % t) for t in range(1, TILES)}
-        nc.scalar.copy(out=windows[0][:, low], in_=acc_low[:])
-        nc.vector.tensor_copy(out=own[0][:, low], in_=acc_low[:])
-        nc.scalar.copy(out=windows[0][:, high], in_=acc_high[:])
-        nc.scalar.copy(out=own[0][:, high], in_=acc_high[:])
-        copy_scores(1, accs[1])
+        def copy_scores(t):
+            nc.scalar.copy(out=windows[t][:], in_=accs[t][:])
+            nc.vector.tensor_copy(out=own[t][:], in_=windows[t][:, low])
 
-        compare(0, 0, halves())
-        compare(0, 1)
-        compare(1, 0)
-        weigh(0, 0)
-        weigh(0, 1)
-        compare(1, 1)
-        copy_scores(2, accs[2])
-        copy_scores(3, accs[3])
-        add_on_tensor(0, "bank_low")
-        compare(2, 0)
-        weigh(1, 0)
-        weigh(1, 1)
-        add_on_tensor(1, "bank_high")
-        compare(2, 1, tag="turned0")
-        compare(3, 0, tag="turned1")
-        weigh(2, 0)
-        weigh(2, 1)
-        compare(3, 1)
-        add_on_vector(2)
-        weigh(3, 0)
-        weigh(3, 1, halves())
-        add_on_vector(3, halves())
+        gather_low(0)
+        gather_high(0, "bank6")
+        copy_scores(2)
+        gather_low(1)
+        gather_high(1, "bank7")
+        sigmoid_low(0)
+        copy_scores(3)
+        gather_low(2)
+        sigmoid_high(0, "bank0")
+        weigh_low(0)
+        sigmoid_high(1, "bank2")
+        gather_low(3)
+        weigh_high(0)
+        finish(0)
+        sigmoid_low(1)
+        gather_high(2, "bank1")
+        weigh_low(1)
+        weigh_high(1)
+        finish(1)
+        sigmoid_low(2)
+        sigmoid_high(2, "bank4")
+        gather_high(3, "bank3")
+        weigh_low(2)
+        weigh_high(2)
+        finish(2)
+        sigmoid_low(3)
+        sigmoid_high(3, "bank5")
+        weigh_low(3)
+        weigh_high(3)
+        finish(3, (low, high))

@@ -34,61 +34,66 @@ def tile_picked_lamrank_none_p_kernel(tc, x_words, x_scales, w1, dg1, dg2, offs,
         p1_sb = keep.tile([P, S // STRIPE], U16, name="p1_sb")
         p2_sb = keep.tile([P, S // STRIPE], U16, name="p2_sb")
         partners = [p1_sb, p2_sb]
-        w_raw = keep.tile([P, PACK, N], F32, name="w_raw")
+        w_raw = keep.tile([P, PACK, N], F32, name="w_raw", tag="w_raw", align_bytes=64)
         scale_table = keep.tile([P, T], U8, name="scale_table", tag="scale_table", align_bytes=64)
-        word_table = keep.tile([P, T], I32, name="word_table", tag="word_table", align_bytes=64)
+        word_table = keep.tile([P, T], I32, name="word_table", align_bytes=64)
         ident = keep.tile([P, P], F32, name="ident")
         windows = [keep.tile([P, S], F32, name="window%d" % t) for t in range(TILES)]
-        gains = [keep.tile([P, SIDES, PAIR, S], F32, name="gain%d" % h) for h in range(TILES // PAIR)]
 
-        nc.vector.memset(scale_table[:].bitcast(I32), 0)
+        nc.gpsimd.memset(scale_table[:].bitcast(I32), 0)
         make_identity(nc, ident[:])
         warm = keep.tile([P, 8], F32, name="warm")
-        nc.scalar.activation(out=warm[:, :1], in_=ident[:, :1], func=ACT.Sigmoid)
+        nc.vector.memset(warm[:, :1], 0.0)
+        nc.scalar.activation(out=warm[:, 1:2], in_=warm[:, :1], func=ACT.Sigmoid)
 
-        nc.sync.dma_start(out=w_raw[:], in_=w1.rearrange("(p j) m -> p j m", j=PACK))
-        for r in range(4):
-            nc.sync.dma_start(out=scale_table[r:P:32, :].bitcast(I32), in_=x_scales[0, r:16:4, :].bitcast(I32))
+        w_rows = w1.rearrange("(p j) m -> p j m", j=PACK)
+        nc.sync.dma_start(out=w_raw[:, :1], in_=w_rows[:, :1])
+        nc.sync.dma_start(out=scale_table[0:P:8, :].bitcast(I32), in_=x_scales[0].bitcast(I32))
         nc.sync.dma_start(out=offs_sb[:], in_=offs)
+        nc.sync.dma_start(out=w_raw[:, 1:2], in_=w_rows[:, 1:2])
+        nc.sync.dma_start(out=w_raw[:, 2:], in_=w_rows[:, 2:])
         nc.sync.dma_start(out=word_table[:], in_=x_words[0].rearrange("p n t -> p (n t)").bitcast(I32))
         nc.sync.dma_start(out=p1_sb[:], in_=p1)
         nc.sync.dma_start(out=p2_sb[:], in_=p2)
-        gain_rows = [dg.rearrange("(p t) j -> p t j", t=TILES) for dg in (dg1, dg2)]
-        for h in range(TILES // PAIR):
-            for side in range(SIDES):
-                nc.sync.dma_start(out=gains[h][:, side], in_=gain_rows[side][:, PAIR * h : PAIR * (h + 1), :])
 
-        w_grouped = [keep.tile([P, PAIR, P, PACK], BF16, name="w_grouped%d" % h, align_bytes=64) for h in range(TILES // PAIR)]
+        x_bytes = keep.tile([P, S], U8, name="x_bytes", align_bytes=64)
+        picked_bytes = keep.tile([P, S], U8, name="picked_bytes", align_bytes=64)
+        nc.gpsimd.memset(x_bytes[:].bitcast(I32), 0)
+        w_grouped = [keep.tile([P, PAIR, P, PACK], BF16, name="w_grouped%d" % h, tag="w_grouped%d" % h, align_bytes=64) for h in range(TILES // PAIR)]
         w_scales = [keep.tile([P, PAIR * P], U8, name="w_scales%d" % h, align_bytes=64) for h in range(TILES // PAIR)]
         dealt = w_raw[:].rearrange("p j (c t) -> p c j t", t=TILES)
         nc.scalar.copy(out=w_grouped[0][:].rearrange("p t c j -> p c j t"), in_=dealt[:, :, :, :PAIR])
+        nc.vector.tensor_copy(out=picked_bytes[:], in_=scale_table[:].indirect(offs_sb[:]))
+        for r in range(4):
+            nc.sync.dma_start(out=x_bytes[r:P:32, :].bitcast(I32), in_=picked_bytes[8 * r : P : 32, :].bitcast(I32))
         nc.vector.tensor_copy(out=w_grouped[1][:].rearrange("p t c j -> p c j t"), in_=dealt[:, :, :, PAIR:])
 
-        x_bytes = keep.tile([P, S], U8, name="x_bytes", align_bytes=64)
-        x_codes = keep.tile([P, S], U32, name="x_codes", align_bytes=64)
-
-        def quantize(h, tag):
-            codes = keep.tile([P, PAIR * P], U32, name="w_codes%d" % h, tag=tag, align_bytes=64)
-            nc.vector.quantize_mx(out=codes[:].bitcast(FP8X4), scales=w_scales[h][:], in_=w_grouped[h][:].rearrange("p t c j -> p (t c j)"))
-            return codes
 
         low, high, whole = slice(0, HALF), slice(HALF, S), slice(0, S)
 
         def entries(list_tile, cols):
             return list_tile[:, cols.start // STRIPE : cols.stop // STRIPE]
 
-        late_codes = quantize(1, "w_codes1")
-        nc.vector.tensor_copy(out=x_bytes[:], in_=scale_table[:].indirect(offs_sb[:]))
-        w_codes = [quantize(0, "scale_table"), late_codes]
+        w_codes = keep.tile([P, N], U32, name="w_codes", align_bytes=64)
+        for h in (1, 0):
+            nc.vector.quantize_mx(out=w_codes[:, h * PAIR * P : (h + 1) * PAIR * P].bitcast(FP8X4), scales=w_scales[h][:], in_=w_grouped[h][:].rearrange("p t c j -> p (t c j)"))
+        x_codes = keep.tile([P, S], U32, name="x_codes", align_bytes=64)
         for cols in (low, high):
             nc.vector.tensor_copy(out=x_codes[:, cols], in_=word_table[:].bitcast(U32).indirect(entries(offs_sb, cols)))
+
+        gain_rows = [dg.rearrange("(p t) j -> p t j", t=TILES) for dg in (dg1, dg2)]
+        gains = []
+        for h, tag in enumerate(("scale_table", "w_raw")):
+            gains.append(keep.tile([P, SIDES, PAIR, S], F32, name="gain%d" % h, tag=tag, align_bytes=64))
+            for side in range(SIDES):
+                nc.sync.dma_start(out=gains[h][:, side], in_=gain_rows[side][:, PAIR * h : PAIR * (h + 1), :])
 
         def multiply(t, cols, bank):
             acc = psum.tile([P, cols.stop - cols.start], F32, name="acc_" + bank, tag=bank)
             rankers = slice(t % PAIR * P, (t % PAIR + 1) * P)
             nc.tensor.matmul_mx(
                 out=acc[:],
-                lhsT=w_codes[t // PAIR][:, rankers].bitcast(FP8X4),
+                lhsT=w_codes[:, t * P : (t + 1) * P].bitcast(FP8X4),
                 lhsT_scale=w_scales[t // PAIR][:, rankers],
                 rhs=x_codes[:, cols].bitcast(FP8X4),
                 rhs_scale=x_bytes[:, cols],
@@ -105,13 +110,14 @@ def tile_picked_lamrank_none_p_kernel(tc, x_words, x_scales, w1, dg1, dg2, offs,
         out_rows = out.rearrange("(p t) j -> p t j", t=TILES)
         sig_low, sig_high, turned = {}, {}, {}
 
-        def gather_low(t):
-            for side in range(SIDES):
+        def gather_low(t, sides=(0, 1)):
+            for side in sides:
                 nc.vector.tensor_tensor(out=diff[t][:, side, :], in0=windows[t][:].indirect(entries(partners[side], low)), in1=own[t][:], op=ALU.subtract)
 
-        def gather_high(t, bank):
-            turned[t] = psum.tile([P, S], F32, name="turned%d" % t, tag=bank)
-            for side in range(SIDES):
+        def gather_high(t, bank, sides=(0, 1)):
+            if t not in turned:
+                turned[t] = psum.tile([P, S], F32, name="turned%d" % t, tag=bank)
+            for side in sides:
                 nc.scalar.activation(out=minus[t][:, side, :], in_=windows[t][:].indirect(entries(partners[side], high)), func=ACT.Copy, scale=-1.0)
                 for b in range(HALF // P):
                     place = turned[t][:, side * HALF + b * P : side * HALF + (b + 1) * P]
@@ -140,14 +146,17 @@ def tile_picked_lamrank_none_p_kernel(tc, x_words, x_scales, w1, dg1, dg2, offs,
                 nc.vector.tensor_tensor(out=result[t][:, cols], in0=product[t][:, 0, cols], in1=product[t][:, 1, cols], op=ALU.add)
                 nc.sync.dma_start(out=out_rows[:, t, cols], in_=result[t][:, cols])
 
-        acc_low = [multiply(t, low, "bank%d" % t) for t in range(PAIR)]
-        acc_high = [multiply(t, high, "bank%d" % (PAIR + t)) for t in range(PAIR)]
-        accs = {t: multiply(t, whole, "bank%d" % (PAIR + t)) for t in range(PAIR, TILES)}
-        for t in range(PAIR):
+        acc_low, acc_high = {}, {}
+        acc_low[0] = multiply(0, low, "bank0")
+        acc_low[1] = multiply(1, low, "bank1")
+        acc_high[0] = multiply(0, high, "bank2")
+        acc_high[1] = multiply(1, high, "bank3")
+        accs = {t: multiply(t, whole, "bank%d" % (2 + t)) for t in (2, 3)}
+        for t in range(2):
             nc.scalar.copy(out=windows[t][:, low], in_=acc_low[t][:])
             nc.vector.tensor_copy(out=own[t][:], in_=acc_low[t][:])
-        for t in range(PAIR):
-            nc.scalar.copy(out=windows[t][:, high], in_=acc_high[t][:])
+        nc.scalar.copy(out=windows[0][:, high], in_=acc_high[0][:])
+        nc.scalar.copy(out=windows[1][:, high], in_=acc_high[1][:])
 
         def copy_scores(t):
             nc.scalar.copy(out=windows[t][:], in_=accs[t][:])
@@ -181,5 +190,6 @@ def tile_picked_lamrank_none_p_kernel(tc, x_words, x_scales, w1, dg1, dg2, offs,
         sigmoid_low(3)
         sigmoid_high(3, "bank5")
         weigh_low(3)
+        finish(3, (low,))
         weigh_high(3)
-        finish(3, (low, high))
+        finish(3, (high,))

@@ -22,6 +22,7 @@ PAIR = 2
 SIDES = 2
 HALF = S // 2
 FLOPS = 2 * K * N * S
+FETCH_TAGS = {(2, 0): "fetched0_0", (3, 0): "fetched1_0"}
 
 
 def tile_picked_lamrank_none_p_kernel(tc, x_words, x_scales, w1, dg1, dg2, offs, p1, p2, out):
@@ -38,7 +39,7 @@ def tile_picked_lamrank_none_p_kernel(tc, x_words, x_scales, w1, dg1, dg2, offs,
         scale_table = keep.tile([P, T], U8, name="scale_table", tag="scale_table", align_bytes=64)
         word_table = keep.tile([P, T], I32, name="word_table", align_bytes=64)
         ident = keep.tile([P, P], F32, name="ident")
-        windows = [keep.tile([P, S], F32, name="window%d" % t) for t in range(TILES)]
+        windows = [keep.tile([P, S], F32, name="window%d" % t) for t in range(PAIR)]
 
         nc.gpsimd.memset(scale_table[:].bitcast(I32), 0)
         make_identity(nc, ident[:])
@@ -102,94 +103,114 @@ def tile_picked_lamrank_none_p_kernel(tc, x_words, x_scales, w1, dg1, dg2, offs,
             )
             return acc
 
-        own = [keep.tile([P, HALF], F32, name="own%d" % t) for t in range(TILES)]
-        diff = [keep.tile([P, SIDES, HALF], F32, name="diff%d" % t) for t in range(TILES)]
-        minus = [keep.tile([P, SIDES, HALF], F32, name="minus%d" % t) for t in range(TILES)]
+        halves = (low, high)
+        own = [keep.tile([P, HALF], F32, name="own%d" % t, tag="own%d" % t) for t in range(2)]
+        fetched = {}
+
+        def fetch_tile(t, h):
+            if (t, h) not in fetched:
+                fetched[(t, h)] = keep.tile([P, SIDES, HALF], F32, name="fetched%d_%d" % (t, h), tag=FETCH_TAGS.get((t, h), "fetched%d_%d" % (t, h)))
+            return fetched[(t, h)]
+
         product = [keep.tile([P, SIDES, S], F32, name="product%d" % t) for t in range(TILES)]
         result = [keep.tile([P, S], F32, name="result%d" % t) for t in range(TILES)]
         out_rows = out.rearrange("(p t) j -> p t j", t=TILES)
-        sig_low, sig_high, turned = {}, {}, {}
+        turned, sigmoids = {}, {}
 
-        def gather_low(t, sides=(0, 1)):
+        def gather_fused(t, sides=(0, 1)):
             for side in sides:
-                nc.vector.tensor_tensor(out=diff[t][:, side, :], in0=windows[t][:].indirect(entries(partners[side], low)), in1=own[t][:], op=ALU.subtract)
+                nc.vector.tensor_tensor(out=fetch_tile(t, 0)[:, side, :], in0=windows[t][:].indirect(entries(partners[side], low)), in1=own[t][:], op=ALU.subtract)
 
-        def gather_high(t, bank, sides=(0, 1)):
-            if t not in turned:
-                turned[t] = psum.tile([P, S], F32, name="turned%d" % t, tag=bank)
+        def gather_plain(t, sides=(0, 1)):
             for side in sides:
-                nc.scalar.activation(out=minus[t][:, side, :], in_=windows[t][:].indirect(entries(partners[side], high)), func=ACT.Copy, scale=-1.0)
+                nc.vector.tensor_copy(out=fetch_tile(t, 0)[:, side, :], in_=windows[t][:].indirect(entries(partners[side], low)))
+
+        def subtract(t):
+            nc.vector.tensor_tensor(out=fetched[(t, 0)][:], in0=fetched[(t, 0)][:], in1=accs[t][:, low].unsqueeze(1).to_broadcast([P, SIDES, HALF]), op=ALU.subtract)
+
+        def gather_turned(t, h, bank, sides=(0, 1)):
+            if (t, h) not in turned:
+                turned[(t, h)] = psum.tile([P, S], F32, name="turned%d_%d" % (t, h), tag=bank)
+                for i in range(S // P):
+                    first = h * HALF + i % 2 * P
+                    nc.tensor.matmul(out=turned[(t, h)][:, i * P : (i + 1) * P], lhsT=windows[t][:, first : first + P], rhs=ident[:], start=(i == 0), stop=False, is_transpose=True)
+            for side in sides:
+                minus = fetch_tile(t, h)[:, side, :]
+                looked_up = windows[t][:].indirect(entries(partners[side], halves[h]))
+                if h == 0:
+                    nc.vector.tensor_scalar(out=minus, in0=looked_up, scalar1=-1.0, scalar2=0.0, op0=ALU.mult, op1=ALU.add)
+                else:
+                    nc.scalar.activation(out=minus, in_=looked_up, func=ACT.Copy, scale=-1.0)
                 for b in range(HALF // P):
-                    place = turned[t][:, side * HALF + b * P : side * HALF + (b + 1) * P]
-                    nc.tensor.matmul(out=place, lhsT=windows[t][:, HALF + b * P : HALF + (b + 1) * P], rhs=ident[:], start=True, stop=False, is_transpose=True)
-                    nc.tensor.matmul(out=place, lhsT=minus[t][:, side, b * P : (b + 1) * P], rhs=ident[:], start=False, stop=True, is_transpose=True)
+                    place = turned[(t, h)][:, side * HALF + b * P : side * HALF + (b + 1) * P]
+                    nc.tensor.matmul(out=place, lhsT=minus[:, b * P : (b + 1) * P], rhs=ident[:], start=False, stop=(side == 1 and b == 1), is_transpose=True)
 
-        def sigmoid_low(t):
-            sig_low[t] = keep.tile([P, SIDES, HALF], F32, name="sig_low%d" % t)
-            nc.scalar.activation(out=sig_low[t][:], in_=diff[t][:], func=ACT.Sigmoid)
+        def sigmoid_fused(t):
+            plain = keep.tile([P, SIDES, HALF], F32, name="sigmoid%d" % t)
+            nc.scalar.activation(out=plain[:], in_=fetched[(t, 0)][:], func=ACT.Sigmoid)
+            sigmoids[(t, 0)] = plain[:]
 
-        def sigmoid_high(t, bank):
-            sig_turned = keep.tile([P, S], F32, name="sig_turned%d" % t)
-            nc.scalar.activation(out=sig_turned[:], in_=turned[t][:], func=ACT.Sigmoid, scale=-1.0)
-            sig_high[t] = psum.tile([P, S], F32, name="sig_high%d" % t, tag=bank)
+        def sigmoid_turned(t, h, bank):
+            sig_turned = keep.tile([P, S], F32, name="sig_turned%d_%d" % (t, h))
+            nc.scalar.activation(out=sig_turned[:], in_=turned[(t, h)][:], func=ACT.Sigmoid, scale=-1.0)
+            back = psum.tile([P, S], F32, name="back%d_%d" % (t, h), tag=bank)
             for b in range(S // P):
-                nc.tensor.transpose(sig_high[t][:, b * P : (b + 1) * P], sig_turned[:, b * P : (b + 1) * P], ident[:])
+                nc.tensor.transpose(back[:, b * P : (b + 1) * P], sig_turned[:, b * P : (b + 1) * P], ident[:])
+            sigmoids[(t, h)] = back[:].rearrange("p (s j) -> p s j", s=SIDES)
 
-        def weigh_low(t):
-            nc.vector.tensor_tensor(out=product[t][:, :, low], in0=sig_low[t][:], in1=gains[t // PAIR][:, :, t % PAIR, low], op=ALU.mult)
+        def weigh(t, h, engine=nc.vector):
+            engine.tensor_tensor(out=product[t][:, :, halves[h]], in0=sigmoids[(t, h)], in1=gains[t // PAIR][:, :, t % PAIR, halves[h]], op=ALU.mult)
 
-        def weigh_high(t):
-            nc.vector.tensor_tensor(out=product[t][:, :, high], in0=sig_high[t][:].rearrange("p (s j) -> p s j", s=SIDES), in1=gains[t // PAIR][:, :, t % PAIR, high], op=ALU.mult)
+        def finish(t, cols=whole, engine=nc.vector):
+            engine.tensor_tensor(out=result[t][:, cols], in0=product[t][:, 0, cols], in1=product[t][:, 1, cols], op=ALU.add)
+            nc.sync.dma_start(out=out_rows[:, t, cols], in_=result[t][:, cols])
 
-        def finish(t, pieces=(whole,)):
-            for cols in pieces:
-                nc.vector.tensor_tensor(out=result[t][:, cols], in0=product[t][:, 0, cols], in1=product[t][:, 1, cols], op=ALU.add)
-                nc.sync.dma_start(out=out_rows[:, t, cols], in_=result[t][:, cols])
-
-        acc_low, acc_high = {}, {}
-        acc_low[0] = multiply(0, low, "bank0")
-        acc_low[1] = multiply(1, low, "bank1")
-        acc_high[0] = multiply(0, high, "bank2")
-        acc_high[1] = multiply(1, high, "bank3")
+        acc_low = [multiply(t, low, "bank%d" % t) for t in range(2)]
+        acc_high = [multiply(t, high, "bank%d" % (2 + t)) for t in range(2)]
         accs = {t: multiply(t, whole, "bank%d" % (2 + t)) for t in (2, 3)}
         for t in range(2):
             nc.scalar.copy(out=windows[t][:, low], in_=acc_low[t][:])
             nc.vector.tensor_copy(out=own[t][:], in_=acc_low[t][:])
-        nc.scalar.copy(out=windows[0][:, high], in_=acc_high[0][:])
-        nc.scalar.copy(out=windows[1][:, high], in_=acc_high[1][:])
+        for t in range(2):
+            nc.scalar.copy(out=windows[t][:, high], in_=acc_high[t][:])
 
         def copy_scores(t):
-            nc.scalar.copy(out=windows[t][:], in_=accs[t][:])
-            nc.vector.tensor_copy(out=own[t][:], in_=windows[t][:, low])
+            windows.append(keep.tile([P, S], F32, name="window%d" % t, tag="own%d" % (t - PAIR)))
+            nc.vector.tensor_copy(out=windows[t][:], in_=accs[t][:])
 
-        gather_low(0)
-        gather_high(0, "bank6")
+        gather_fused(0)
+        gather_turned(0, 1, "bank6")
+        gather_fused(1)
+        sigmoid_fused(0)
         copy_scores(2)
-        gather_low(1)
-        gather_high(1, "bank7")
-        sigmoid_low(0)
         copy_scores(3)
-        gather_low(2)
-        sigmoid_high(0, "bank0")
-        weigh_low(0)
-        sigmoid_high(1, "bank2")
-        gather_low(3)
-        weigh_high(0)
-        finish(0)
-        sigmoid_low(1)
-        gather_high(2, "bank1")
-        weigh_low(1)
-        weigh_high(1)
-        finish(1)
-        sigmoid_low(2)
-        sigmoid_high(2, "bank4")
-        gather_high(3, "bank3")
-        weigh_low(2)
-        weigh_high(2)
+        weigh(0, 0, nc.gpsimd)
+        gather_turned(1, 1, "bank7", (0,))
+        sigmoid_turned(0, 1, "bank0")
+        sigmoid_fused(1)
+        gather_plain(2)
+        weigh(1, 0, nc.gpsimd)
+        gather_turned(1, 1, "bank7", (1,))
+        weigh(0, 1)
+        subtract(2)
+        finish(0, whole, nc.gpsimd)
+        gather_turned(2, 1, "bank1", (0,))
+        sigmoid_turned(1, 1, "bank2")
+        gather_plain(3)
+        gather_turned(2, 1, "bank1", (1,))
+        sigmoid_fused(2)
+        weigh(1, 1)
+        subtract(3)
+        weigh(2, 0, nc.gpsimd)
+        finish(1, whole, nc.gpsimd)
+        gather_turned(3, 1, "bank3", (0,))
+        sigmoid_turned(2, 1, "bank6")
+        gather_turned(3, 1, "bank3", (1,))
+        sigmoid_fused(3)
+        sigmoid_turned(3, 1, "bank4")
+        weigh(2, 1)
+        weigh(3, 0)
         finish(2)
-        sigmoid_low(3)
-        sigmoid_high(3, "bank5")
-        weigh_low(3)
-        finish(3, (low,))
-        weigh_high(3)
-        finish(3, (high,))
+        weigh(3, 1)
+        finish(3, low)
+        finish(3, high)

@@ -22,13 +22,14 @@ PAIR = 2
 SIDES = 2
 HALF = S // 2
 FLOPS = 2 * K * N * S
-FETCH_TAGS = {(2, 0): "fetched0_0", (3, 0): "fetched1_0"}
+PLACES = {"window2": 0, "own0": 1536, "window3": 2048, "product_low": "own1", "result0_1": 5632, "sigmoid1": 6144, "fetched3_0": 7168, "sigmoid3": "fetched3_1", "diff2": "sig_turned0_1", "diff3": "sig_turned1_1", "product1_1": 10240, "result2_0": 11264, "sig_turned3_1": 12288, "product3_0": 13312}
 
 
 def tile_picked_lamrank_none_p_kernel(tc, x_words, x_scales, w1, dg1, dg2, offs, p1, p2, out):
     nc = tc.nc
     with ExitStack() as ctx:
         keep = ctx.enter_context(tc.tile_pool(name="keep", bufs=1))
+        shared = ctx.enter_context(tc.tile_pool(name="shared", bufs=1))
         psum = ctx.enter_context(tc.psum_pool(name="psum", bufs=1))
 
         offs_sb = keep.tile([P, S // STRIPE], U16, name="offs_sb")
@@ -104,40 +105,48 @@ def tile_picked_lamrank_none_p_kernel(tc, x_words, x_scales, w1, dg1, dg2, offs,
             return acc
 
         halves = (low, high)
-        own = [keep.tile([P, HALF], F32, name="own%d" % t, tag="own%d" % t) for t in range(2)]
-        fetched = {}
+
+        def scratch(name, shape):
+            place = PLACES.get(name, name)
+            if isinstance(place, int):
+                return shared.tile(shape, F32, name=name, offset=place)
+            return keep.tile(shape, F32, name=name, tag=place)
+
+        own = [scratch("own%d" % t, [P, HALF]) for t in range(PAIR)]
+        out_rows = out.rearrange("(p t) j -> p t j", t=TILES)
+        fetched, turned, sigmoids, diffs, product, result = {}, {}, {}, {}, {}, {}
 
         def fetch_tile(t, h):
             if (t, h) not in fetched:
-                fetched[(t, h)] = keep.tile([P, SIDES, HALF], F32, name="fetched%d_%d" % (t, h), tag=FETCH_TAGS.get((t, h), "fetched%d_%d" % (t, h)))
+                fetched[(t, h)] = scratch("fetched%d_%d" % (t, h), [P, SIDES, HALF])
             return fetched[(t, h)]
-
-        product = [keep.tile([P, SIDES, S], F32, name="product%d" % t) for t in range(TILES)]
-        result = [keep.tile([P, S], F32, name="result%d" % t) for t in range(TILES)]
-        out_rows = out.rearrange("(p t) j -> p t j", t=TILES)
-        turned, sigmoids = {}, {}
 
         def gather_fused(t, sides=(0, 1)):
             for side in sides:
                 nc.vector.tensor_tensor(out=fetch_tile(t, 0)[:, side, :], in0=windows[t][:].indirect(entries(partners[side], low)), in1=own[t][:], op=ALU.subtract)
+            diffs[t] = fetched[(t, 0)]
 
         def gather_plain(t, sides=(0, 1)):
             for side in sides:
                 nc.vector.tensor_copy(out=fetch_tile(t, 0)[:, side, :], in_=windows[t][:].indirect(entries(partners[side], low)))
 
         def subtract(t):
-            nc.vector.tensor_tensor(out=fetched[(t, 0)][:], in0=fetched[(t, 0)][:], in1=accs[t][:, low].unsqueeze(1).to_broadcast([P, SIDES, HALF]), op=ALU.subtract)
+            diffs[t] = scratch("diff%d" % t, [P, SIDES, HALF])
+            nc.vector.tensor_tensor(out=diffs[t][:], in0=fetched[(t, 0)][:], in1=accs[t][:, low].unsqueeze(1).to_broadcast([P, SIDES, HALF]), op=ALU.subtract)
 
-        def gather_turned(t, h, bank, sides=(0, 1)):
+        def turn_own(t, h, bank):
+            turned[(t, h)] = psum.tile([P, S], F32, name="turned%d_%d" % (t, h), tag=bank)
+            for i in range(S // P):
+                first = h * HALF + i % 2 * P
+                nc.tensor.matmul(out=turned[(t, h)][:, i * P : (i + 1) * P], lhsT=windows[t][:, first : first + P], rhs=ident[:], start=(i == 0), stop=False, is_transpose=True)
+
+        def gather_turned(t, h, bank, sides=(0, 1), on_vector=False):
             if (t, h) not in turned:
-                turned[(t, h)] = psum.tile([P, S], F32, name="turned%d_%d" % (t, h), tag=bank)
-                for i in range(S // P):
-                    first = h * HALF + i % 2 * P
-                    nc.tensor.matmul(out=turned[(t, h)][:, i * P : (i + 1) * P], lhsT=windows[t][:, first : first + P], rhs=ident[:], start=(i == 0), stop=False, is_transpose=True)
+                turn_own(t, h, bank)
             for side in sides:
                 minus = fetch_tile(t, h)[:, side, :]
                 looked_up = windows[t][:].indirect(entries(partners[side], halves[h]))
-                if h == 0:
+                if on_vector:
                     nc.vector.tensor_scalar(out=minus, in0=looked_up, scalar1=-1.0, scalar2=0.0, op0=ALU.mult, op1=ALU.add)
                 else:
                     nc.scalar.activation(out=minus, in_=looked_up, func=ACT.Copy, scale=-1.0)
@@ -145,13 +154,13 @@ def tile_picked_lamrank_none_p_kernel(tc, x_words, x_scales, w1, dg1, dg2, offs,
                     place = turned[(t, h)][:, side * HALF + b * P : side * HALF + (b + 1) * P]
                     nc.tensor.matmul(out=place, lhsT=minus[:, b * P : (b + 1) * P], rhs=ident[:], start=False, stop=(side == 1 and b == 1), is_transpose=True)
 
-        def sigmoid_fused(t):
-            plain = keep.tile([P, SIDES, HALF], F32, name="sigmoid%d" % t)
-            nc.scalar.activation(out=plain[:], in_=fetched[(t, 0)][:], func=ACT.Sigmoid)
+        def sigmoid_low(t):
+            plain = scratch("sigmoid%d" % t, [P, SIDES, HALF])
+            nc.scalar.activation(out=plain[:], in_=diffs[t][:], func=ACT.Sigmoid)
             sigmoids[(t, 0)] = plain[:]
 
         def sigmoid_turned(t, h, bank):
-            sig_turned = keep.tile([P, S], F32, name="sig_turned%d_%d" % (t, h))
+            sig_turned = scratch("sig_turned%d_%d" % (t, h), [P, S])
             nc.scalar.activation(out=sig_turned[:], in_=turned[(t, h)][:], func=ACT.Sigmoid, scale=-1.0)
             back = psum.tile([P, S], F32, name="back%d_%d" % (t, h), tag=bank)
             for b in range(S // P):
@@ -159,11 +168,26 @@ def tile_picked_lamrank_none_p_kernel(tc, x_words, x_scales, w1, dg1, dg2, offs,
             sigmoids[(t, h)] = back[:].rearrange("p (s j) -> p s j", s=SIDES)
 
         def weigh(t, h, engine=nc.vector):
-            engine.tensor_tensor(out=product[t][:, :, halves[h]], in0=sigmoids[(t, h)], in1=gains[t // PAIR][:, :, t % PAIR, halves[h]], op=ALU.mult)
+            if (t, h) not in product:
+                if (t, h) == (0, 0):
+                    both = scratch("product_low", [P, PAIR, SIDES, HALF])
+                    product[(0, 0)], product[(1, 0)], product["both"] = both[:, 0], both[:, 1], both
+                else:
+                    product[(t, h)] = scratch("product%d_%d" % (t, h), [P, SIDES, HALF])[:]
+            engine.tensor_tensor(out=product[(t, h)], in0=sigmoids[(t, h)], in1=gains[t // PAIR][:, :, t % PAIR, halves[h]], op=ALU.mult)
 
-        def finish(t, cols=whole, engine=nc.vector):
-            engine.tensor_tensor(out=result[t][:, cols], in0=product[t][:, 0, cols], in1=product[t][:, 1, cols], op=ALU.add)
-            nc.sync.dma_start(out=out_rows[:, t, cols], in_=result[t][:, cols])
+        def finish_both(engine):
+            summed = scratch("result_low", [P, PAIR, HALF])
+            engine.tensor_tensor(out=summed[:], in0=product["both"][:, :, 0], in1=product["both"][:, :, 1], op=ALU.add)
+            nc.sync.dma_start(out=out_rows[:, :PAIR, low], in_=summed[:])
+
+        def finish(t, h, engine=nc.vector):
+            key = (t, 0 if t == 2 else h)
+            if key not in result:
+                result[key] = scratch("result%d_%d" % key, [P, S if t == 2 else HALF])
+            summed = result[key][:, halves[h]] if t == 2 else result[key][:]
+            engine.tensor_tensor(out=summed, in0=product[(t, h)][:, 0], in1=product[(t, h)][:, 1], op=ALU.add)
+            nc.sync.dma_start(out=out_rows[:, t, halves[h]], in_=summed)
 
         acc_low = [multiply(t, low, "bank%d" % t) for t in range(2)]
         acc_high = [multiply(t, high, "bank%d" % (2 + t)) for t in range(2)]
@@ -175,42 +199,43 @@ def tile_picked_lamrank_none_p_kernel(tc, x_words, x_scales, w1, dg1, dg2, offs,
             nc.scalar.copy(out=windows[t][:, high], in_=acc_high[t][:])
 
         def copy_scores(t):
-            windows.append(keep.tile([P, S], F32, name="window%d" % t, tag="own%d" % (t - PAIR)))
+            windows.append(scratch("window%d" % t, [P, S]))
             nc.vector.tensor_copy(out=windows[t][:], in_=accs[t][:])
 
         gather_fused(0)
         gather_turned(0, 1, "bank6")
         gather_fused(1)
-        sigmoid_fused(0)
-        copy_scores(2)
-        copy_scores(3)
-        weigh(0, 0, nc.gpsimd)
         gather_turned(1, 1, "bank7", (0,))
+        sigmoid_low(0)
+        copy_scores(2)
+        weigh(0, 0, nc.gpsimd)
         sigmoid_turned(0, 1, "bank0")
-        sigmoid_fused(1)
+        sigmoid_low(1)
+        gather_turned(1, 1, "bank7", (1,), True)
+        copy_scores(3)
         gather_plain(2)
         weigh(1, 0, nc.gpsimd)
-        gather_turned(1, 1, "bank7", (1,))
         weigh(0, 1)
         subtract(2)
-        finish(0, whole, nc.gpsimd)
-        gather_turned(2, 1, "bank1", (0,))
+        finish_both(nc.gpsimd)
+        gather_turned(2, 1, "bank1")
+        turn_own(3, 1, "bank3")
         sigmoid_turned(1, 1, "bank2")
+        finish(0, 1, nc.gpsimd)
         gather_plain(3)
-        gather_turned(2, 1, "bank1", (1,))
-        sigmoid_fused(2)
+        gather_turned(3, 1, "bank3")
+        sigmoid_low(2)
         weigh(1, 1)
         subtract(3)
         weigh(2, 0, nc.gpsimd)
-        finish(1, whole, nc.gpsimd)
-        gather_turned(3, 1, "bank3", (0,))
+        finish(1, 1, nc.gpsimd)
         sigmoid_turned(2, 1, "bank6")
-        gather_turned(3, 1, "bank3", (1,))
-        sigmoid_fused(3)
         sigmoid_turned(3, 1, "bank4")
+        sigmoid_low(3)
         weigh(2, 1)
-        weigh(3, 0)
-        finish(2)
         weigh(3, 1)
-        finish(3, low)
-        finish(3, high)
+        finish(2, 1)
+        weigh(3, 0)
+        finish(2, 0)
+        finish(3, 1)
+        finish(3, 0)

@@ -22,7 +22,7 @@ PAIR = 2
 SIDES = 2
 HALF = S // 2
 FLOPS = 2 * K * N * S
-PLACES = {"window2": 0, "own0": 1536, "window3": 2048, "product_low": "own1", "result0_1": 5632, "sigmoid1": 6144, "fetched3_0": 7168, "sigmoid3": "fetched3_1", "diff2": "sig_turned0_1", "diff3": "sig_turned1_1", "product1_1": 10240, "result2_0": 11264, "sig_turned3_1": 12288, "product3_0": 13312}
+PLACES = {"window2": 0, "own0": 1536, "window3": 2048, "product_low": "own1", "fetched3_0": "sig_turned0_0", "result0_1": "sigmoid1", "sigmoid3": "sig_turned1_0", "row2": "sig_turned3_0", "product3_0": "sig_turned3_1", "row3": "product2_1"}
 
 
 def tile_picked_lamrank_none_p_kernel(tc, x_words, x_scales, w1, dg1, dg2, offs, p1, p2, out):
@@ -112,9 +112,10 @@ def tile_picked_lamrank_none_p_kernel(tc, x_words, x_scales, w1, dg1, dg2, offs,
                 return shared.tile(shape, F32, name=name, offset=place)
             return keep.tile(shape, F32, name=name, tag=place)
 
+        rows = {}
         own = [scratch("own%d" % t, [P, HALF]) for t in range(PAIR)]
         out_rows = out.rearrange("(p t) j -> p t j", t=TILES)
-        fetched, turned, sigmoids, diffs, product, result = {}, {}, {}, {}, {}, {}
+        fetched, turned, sigmoids, diffs, product, gains_turned, back = {}, {}, {}, {}, {}, {}, {}
 
         def fetch_tile(t, h):
             if (t, h) not in fetched:
@@ -132,40 +133,84 @@ def tile_picked_lamrank_none_p_kernel(tc, x_words, x_scales, w1, dg1, dg2, offs,
 
         def subtract(t):
             diffs[t] = scratch("diff%d" % t, [P, SIDES, HALF])
-            nc.vector.tensor_tensor(out=diffs[t][:], in0=fetched[(t, 0)][:], in1=accs[t][:, low].unsqueeze(1).to_broadcast([P, SIDES, HALF]), op=ALU.subtract)
+            for side in range(SIDES):
+                nc.vector.tensor_tensor(out=diffs[t][:, side], in0=fetched[(t, 0)][:, side], in1=accs[t][:, low], op=ALU.subtract)
 
         def turn_own(t, h, bank):
             turned[(t, h)] = psum.tile([P, S], F32, name="turned%d_%d" % (t, h), tag=bank)
             for i in range(S // P):
-                first = h * HALF + i % 2 * P
+                first = h * HALF + i // SIDES * P
                 nc.tensor.matmul(out=turned[(t, h)][:, i * P : (i + 1) * P], lhsT=windows[t][:, first : first + P], rhs=ident[:], start=(i == 0), stop=False, is_transpose=True)
 
-        def gather_turned(t, h, bank, sides=(0, 1), on_vector=False):
-            if (t, h) not in turned:
-                turn_own(t, h, bank)
-            for side in sides:
-                minus = fetch_tile(t, h)[:, side, :]
-                looked_up = windows[t][:].indirect(entries(partners[side], halves[h]))
-                if on_vector:
-                    nc.vector.tensor_scalar(out=minus, in0=looked_up, scalar1=-1.0, scalar2=0.0, op0=ALU.mult, op1=ALU.add)
-                else:
-                    nc.scalar.activation(out=minus, in_=looked_up, func=ACT.Copy, scale=-1.0)
-                for b in range(HALF // P):
-                    place = turned[(t, h)][:, side * HALF + b * P : side * HALF + (b + 1) * P]
-                    nc.tensor.matmul(out=place, lhsT=minus[:, b * P : (b + 1) * P], rhs=ident[:], start=False, stop=(side == 1 and b == 1), is_transpose=True)
+        def subtract_on_gpsimd(t):
+            diffs[t] = scratch("diff%d" % t, [P, SIDES, HALF])
+            nc.gpsimd.tensor_tensor(out=diffs[t][:], in0=fetched[(t, 0)][:], in1=windows[t][:, low].unsqueeze(1).to_broadcast([P, SIDES, HALF]), op=ALU.subtract)
+
+        def gather_high(t, side, on_vector=False):
+            minus = fetch_tile(t, 1)[:, side, :]
+            looked_up = windows[t][:].indirect(entries(partners[side], high))
+            if on_vector:
+                nc.vector.tensor_scalar(out=minus, in0=looked_up, scalar1=-1.0, scalar2=0.0, op0=ALU.mult, op1=ALU.add)
+            else:
+                nc.scalar.activation(out=minus, in_=looked_up, func=ACT.Copy, scale=-1.0)
+
+        def turn_fetched(t, side):
+            for b in range(HALF // P):
+                place = turned[(t, 1)][:, (b * SIDES + side) * P : (b * SIDES + side + 1) * P]
+                nc.tensor.matmul(out=place, lhsT=fetched[(t, 1)][:, side, b * P : (b + 1) * P], rhs=ident[:], start=False, stop=(side == 1 and b == 1), is_transpose=True)
 
         def sigmoid_low(t):
             plain = scratch("sigmoid%d" % t, [P, SIDES, HALF])
             nc.scalar.activation(out=plain[:], in_=diffs[t][:], func=ACT.Sigmoid)
             sigmoids[(t, 0)] = plain[:]
 
-        def sigmoid_turned(t, h, bank):
-            sig_turned = scratch("sig_turned%d_%d" % (t, h), [P, S])
-            nc.scalar.activation(out=sig_turned[:], in_=turned[(t, h)][:], func=ACT.Sigmoid, scale=-1.0)
-            back = psum.tile([P, S], F32, name="back%d_%d" % (t, h), tag=bank)
-            for b in range(S // P):
-                nc.tensor.transpose(back[:, b * P : (b + 1) * P], sig_turned[:, b * P : (b + 1) * P], ident[:])
-            sigmoids[(t, h)] = back[:].rearrange("p (s j) -> p s j", s=SIDES)
+        def sigmoid_turned(t, blocks=(0, 1)):
+            sigmoids[(t, 1, blocks)] = scratch("sig_turned%d_%d" % (t, blocks[0]), [P, len(blocks) * SIDES * P])
+            nc.scalar.activation(out=sigmoids[(t, 1, blocks)][:], in_=turned[(t, 1)][:, blocks[0] * SIDES * P : (blocks[-1] + 1) * SIDES * P], func=ACT.Sigmoid, scale=-1.0)
+
+        def turn_sigmoids(t, bank):
+            plain = psum.tile([P, SIDES, HALF], F32, name="sig_back%d" % t, tag=bank)
+            for i in range(S // P):
+                b, side = divmod(i, SIDES)
+                nc.tensor.transpose(plain[:, side, b * P : (b + 1) * P], sigmoids[(t, 1, (0, 1))][:, i * P : (i + 1) * P], ident[:])
+            sigmoids[(t, 1)] = plain[:]
+
+        def turn_gains(t, bank):
+            gains_turned[t] = psum.tile([P, S], F32, name="gains_turned%d" % t, tag=bank)
+            for i in range(S // P):
+                first = HALF + i // SIDES * P
+                nc.tensor.transpose(gains_turned[t][:, i * P : (i + 1) * P], gains[t // PAIR][:, i % SIDES, t % PAIR, first : first + P], ident[:])
+
+        def weigh_turned(t, blocks=(0, 1)):
+            if (t, 1) not in product:
+                product[(t, 1)] = scratch("product%d_1" % t, [P, S])
+            cols = slice(blocks[0] * SIDES * P, (blocks[-1] + 1) * SIDES * P)
+            nc.vector.tensor_tensor(out=product[(t, 1)][:, cols], in0=sigmoids[(t, 1, blocks)][:] if (t, 1, blocks) in sigmoids else sigmoids[(t, 1, (0, 1))][:, cols], in1=gains_turned[t][:, cols], op=ALU.mult)
+
+        def turn_back(t, bank, blocks=(0, 1)):
+            back[(t, blocks[0])] = psum.tile([P, len(blocks) * P], F32, name="back%d_%d" % (t, blocks[0]), tag=bank)
+            for i, b in enumerate(blocks):
+                for side in range(SIDES):
+                    first = (b * SIDES + side) * P
+                    nc.tensor.matmul(out=back[(t, blocks[0])][:, i * P : (i + 1) * P], lhsT=product[(t, 1)][:, first : first + P], rhs=ident[:], start=(side == 0), stop=(side == 1), is_transpose=True)
+
+        def weigh_and_turn(t, bank):
+            back[(t, 0)] = psum.tile([P, HALF], F32, name="back%d" % t, tag=bank)
+            for b in range(HALF // P):
+                weigh_turned(t, (b,))
+                for side in range(SIDES):
+                    first = (b * SIDES + side) * P
+                    nc.tensor.matmul(out=back[(t, 0)][:, b * P : (b + 1) * P], lhsT=product[(t, 1)][:, first : first + P], rhs=ident[:], start=(side == 0), stop=(side == 1), is_transpose=True)
+
+        def finish_turned(t, blocks=(0, 1), on_vector=False):
+            summed = rows[t][:, HALF + blocks[0] * P : HALF + (blocks[-1] + 1) * P] if t in rows else scratch("result%d_1_%d" % (t, blocks[0]), [P, len(blocks) * P])
+            if on_vector:
+                nc.vector.tensor_copy(out=summed[:, :], in_=back[(t, blocks[0])][:])
+            else:
+                nc.scalar.copy(out=summed[:, :], in_=back[(t, blocks[0])][:])
+            queue = nc.scalar if blocks == (1,) else nc.sync
+            if t not in rows:
+                queue.dma_start(out=out_rows[:, t, HALF + blocks[0] * P : HALF + (blocks[-1] + 1) * P], in_=summed[:])
 
         def weigh(t, h, engine=nc.vector):
             if (t, h) not in product:
@@ -182,12 +227,27 @@ def tile_picked_lamrank_none_p_kernel(tc, x_words, x_scales, w1, dg1, dg2, offs,
             nc.sync.dma_start(out=out_rows[:, :PAIR, low], in_=summed[:])
 
         def finish(t, h, engine=nc.vector):
-            key = (t, 0 if t == 2 else h)
-            if key not in result:
-                result[key] = scratch("result%d_%d" % key, [P, S if t == 2 else HALF])
-            summed = result[key][:, halves[h]] if t == 2 else result[key][:]
+            summed = rows[t][:, halves[h]] if t in rows else scratch("result%d_%d" % (t, h), [P, HALF])[:]
             engine.tensor_tensor(out=summed, in0=product[(t, h)][:, 0], in1=product[(t, h)][:, 1], op=ALU.add)
-            nc.sync.dma_start(out=out_rows[:, t, halves[h]], in_=summed)
+            if t not in rows:
+                nc.sync.dma_start(out=out_rows[:, t, halves[h]], in_=summed)
+
+        def finish_last(t):
+            made = scratch("product%d_0" % t, [P, SIDES, HALF])
+            summed = rows[t] if t in rows else scratch("result%d_0" % t, [P, HALF])
+            blocks = [slice(b * P, (b + 1) * P) for b in range(HALF // P)]
+            for cols in blocks:
+                nc.vector.tensor_tensor(out=made[:, :, cols], in0=sigmoids[(t, 0)][:, :, cols], in1=gains[t // PAIR][:, :, t % PAIR, cols], op=ALU.mult)
+            for cols in blocks:
+                nc.vector.tensor_tensor(out=summed[:, cols], in0=made[:, 0, cols], in1=made[:, 1, cols], op=ALU.add)
+            if t not in rows:
+                nc.sync.dma_start(out=out_rows[:, t, low], in_=summed[:])
+
+        def open_row(t):
+            rows[t] = scratch("row%d" % t, [P, S])
+
+        def store_row(t):
+            nc.sync.dma_start(out=out_rows[:, t, :], in_=rows[t][:])
 
         acc_low = [multiply(t, low, "bank%d" % t) for t in range(2)]
         acc_high = [multiply(t, high, "bank%d" % (2 + t)) for t in range(2)]
@@ -203,39 +263,65 @@ def tile_picked_lamrank_none_p_kernel(tc, x_words, x_scales, w1, dg1, dg2, offs,
             nc.vector.tensor_copy(out=windows[t][:], in_=accs[t][:])
 
         gather_fused(0)
-        gather_turned(0, 1, "bank6")
+        gather_high(0, 0)
+        gather_high(0, 1)
+        turn_own(0, 1, "bank6")
+        turn_fetched(0, 0)
+        turn_own(1, 1, "bank7")
+        turn_fetched(0, 1)
         gather_fused(1)
-        gather_turned(1, 1, "bank7", (0,))
+        gather_high(1, 0)
+        turn_fetched(1, 0)
         sigmoid_low(0)
         copy_scores(2)
         weigh(0, 0, nc.gpsimd)
-        sigmoid_turned(0, 1, "bank0")
+        gather_high(1, 1)
         sigmoid_low(1)
-        gather_turned(1, 1, "bank7", (1,), True)
+        sigmoid_turned(0)
+        turn_fetched(1, 1)
+        turn_own(2, 1, "bank1")
+        turn_sigmoids(0, "bank0")
         copy_scores(3)
         gather_plain(2)
         weigh(1, 0, nc.gpsimd)
-        weigh(0, 1)
         subtract(2)
+        weigh(0, 1)
         finish_both(nc.gpsimd)
-        gather_turned(2, 1, "bank1")
-        turn_own(3, 1, "bank3")
-        sigmoid_turned(1, 1, "bank2")
         finish(0, 1, nc.gpsimd)
-        gather_plain(3)
-        gather_turned(3, 1, "bank3")
+        gather_high(2, 0)
+        gather_high(2, 1)
+        turn_fetched(2, 0)
+        turn_own(3, 1, "bank3")
+        turn_fetched(2, 1)
+        gather_high(3, 0)
+        gather_high(3, 1)
+        turn_fetched(3, 0)
+        turn_gains(1, "bank2")
+        turn_fetched(3, 1)
+        turn_gains(2, "bank6")
+        turn_gains(3, "bank4")
         sigmoid_low(2)
-        weigh(1, 1)
+        sigmoid_turned(1)
+        gather_plain(3)
         subtract(3)
         weigh(2, 0, nc.gpsimd)
-        finish(1, 1, nc.gpsimd)
-        sigmoid_turned(2, 1, "bank6")
-        sigmoid_turned(3, 1, "bank4")
+        sigmoid_turned(2)
+        weigh_and_turn(1, "bank7")
+        sigmoid_turned(3, (0,))
+        sigmoid_turned(3, (1,))
         sigmoid_low(3)
-        weigh(2, 1)
-        weigh(3, 1)
-        finish(2, 1)
-        weigh(3, 0)
+        finish_turned(1)
+        weigh_and_turn(2, "bank0")
+        weigh_turned(3, (0,))
+        turn_back(3, "bank1", (0,))
+        weigh_turned(3, (1,))
+        turn_back(3, "bank5", (1,))
+        open_row(2)
         finish(2, 0)
-        finish(3, 1)
-        finish(3, 0)
+        finish_turned(2)
+        store_row(2)
+        open_row(3)
+        finish_turned(3, (0,))
+        finish_last(3)
+        finish_turned(3, (1,))
+        store_row(3)

from contextlib import ExitStack

import concourse.mybir as mybir
from concourse.masks import make_identity

F32 = mybir.dt.float32
BF16 = mybir.dt.bfloat16
I32 = mybir.dt.int32
U32 = mybir.dt.uint32
U16 = mybir.dt.uint16
U8 = mybir.dt.uint8
FP8X4 = mybir.dt.float8_e4m3fn_x4
ALU = mybir.AluOpType
ACT = mybir.ActivationFunctionType

P = 128
PACK = 4
STRIPE = 16
K, T, S, N = 512, 2048, 512, 512
TILES = N // P
PAIR = 2
SIDES = 2
HALF = S // 2
FLOPS = 2 * K * N * S
PLACES = {"window2": 0, "own0": 1536, "window3": 2048, "product_low": "own1", "fetched3_0": "sig_turned0_0", "result0_1": "sigmoid1", "sigmoid3": "sig_turned1_0", "row2": "sig_turned3_0", "product3_0": "sig_turned3_1", "row3": "product2_1"}


def tile_picked_lamrank_none_p_kernel(tc, x_words, x_scales, w1, dg1, dg2, offs, p1, p2, out):
    nc = tc.nc
    with ExitStack() as ctx:
        keep = ctx.enter_context(tc.tile_pool(name="keep", bufs=1))
        shared = ctx.enter_context(tc.tile_pool(name="shared", bufs=1))
        psum = ctx.enter_context(tc.psum_pool(name="psum", bufs=1))

        offs_sb = keep.tile([P, S // STRIPE], U16, name="offs_sb")
        p1_sb = keep.tile([P, S // STRIPE], U16, name="p1_sb")
        p2_sb = keep.tile([P, S // STRIPE], U16, name="p2_sb")
        partners = [p1_sb, p2_sb]
        w_raw = keep.tile([P, PACK, N], F32, name="w_raw", tag="w_raw", align_bytes=64)
        scale_table = keep.tile([P, T], U8, name="scale_table", tag="scale_table", align_bytes=64)
        word_table = keep.tile([P, T], I32, name="word_table", align_bytes=64)
        ident = keep.tile([P, P], F32, name="ident")
        windows = [keep.tile([P, S], F32, name="window%d" % t) for t in range(PAIR)]

        nc.gpsimd.memset(scale_table[:].bitcast(I32), 0)
        make_identity(nc, ident[:])
        warm = keep.tile([P, 8], F32, name="warm")
        nc.vector.memset(warm[:, :1], 0.0)
        nc.scalar.activation(out=warm[:, 1:2], in_=warm[:, :1], func=ACT.Sigmoid)

        w_rows = w1.rearrange("(p j) m -> p j m", j=PACK)
        nc.sync.dma_start(out=w_raw[:, :1], in_=w_rows[:, :1])
        nc.sync.dma_start(out=scale_table[0:P:8, :].bitcast(I32), in_=x_scales[0].bitcast(I32))
        nc.sync.dma_start(out=offs_sb[:], in_=offs)
        nc.sync.dma_start(out=w_raw[:, 1:2], in_=w_rows[:, 1:2])
        nc.sync.dma_start(out=w_raw[:, 2:], in_=w_rows[:, 2:])
        nc.sync.dma_start(out=word_table[:], in_=x_words[0].rearrange("p n t -> p (n t)").bitcast(I32))
        nc.sync.dma_start(out=p1_sb[:], in_=p1)
        nc.sync.dma_start(out=p2_sb[:], in_=p2)

        x_bytes = keep.tile([P, S], U8, name="x_bytes", align_bytes=64)
        picked_bytes = keep.tile([P, S], U8, name="picked_bytes", align_bytes=64)
        nc.gpsimd.memset(x_bytes[:].bitcast(I32), 0)
        w_grouped = [keep.tile([P, PAIR, P, PACK], BF16, name="w_grouped%d" % h, tag="w_grouped%d" % h, align_bytes=64) for h in range(TILES // PAIR)]
        w_scales = [keep.tile([P, PAIR * P], U8, name="w_scales%d" % h, align_bytes=64) for h in range(TILES // PAIR)]
        dealt = w_raw[:].rearrange("p j (c t) -> p c j t", t=TILES)
        nc.scalar.copy(out=w_grouped[0][:].rearrange("p t c j -> p c j t"), in_=dealt[:, :, :, :PAIR])
        nc.vector.tensor_copy(out=picked_bytes[:], in_=scale_table[:].indirect(offs_sb[:]))
        for r in range(4):
            nc.sync.dma_start(out=x_bytes[r:P:32, :].bitcast(I32), in_=picked_bytes[8 * r : P : 32, :].bitcast(I32))
        nc.vector.tensor_copy(out=w_grouped[1][:].rearrange("p t c j -> p c j t"), in_=dealt[:, :, :, PAIR:])


        low, high, whole = slice(0, HALF), slice(HALF, S), slice(0, S)

        def entries(list_tile, cols):
            return list_tile[:, cols.start // STRIPE : cols.stop // STRIPE]

        w_codes = keep.tile([P, N], U32, name="w_codes", align_bytes=64)
        for h in (1, 0):
            nc.vector.quantize_mx(out=w_codes[:, h * PAIR * P : (h + 1) * PAIR * P].bitcast(FP8X4), scales=w_scales[h][:], in_=w_grouped[h][:].rearrange("p t c j -> p (t c j)"))
        x_codes = keep.tile([P, S], U32, name="x_codes", align_bytes=64)
        for cols in (low, high):
            nc.vector.tensor_copy(out=x_codes[:, cols], in_=word_table[:].bitcast(U32).indirect(entries(offs_sb, cols)))

        gain_rows = [dg.rearrange("(p t) j -> p t j", t=TILES) for dg in (dg1, dg2)]
        gains = []
        for h, tag in enumerate(("scale_table", "w_raw")):
            gains.append(keep.tile([P, SIDES, PAIR, S], F32, name="gain%d" % h, tag=tag, align_bytes=64))
            for side in range(SIDES):
                nc.sync.dma_start(out=gains[h][:, side], in_=gain_rows[side][:, PAIR * h : PAIR * (h + 1), :])

        def multiply(t, cols, bank):
            acc = psum.tile([P, cols.stop - cols.start], F32, name="acc_" + bank, tag=bank)
            rankers = slice(t % PAIR * P, (t % PAIR + 1) * P)
            nc.tensor.matmul_mx(
                out=acc[:],
                lhsT=w_codes[:, t * P : (t + 1) * P].bitcast(FP8X4),
                lhsT_scale=w_scales[t // PAIR][:, rankers],
                rhs=x_codes[:, cols].bitcast(FP8X4),
                rhs_scale=x_bytes[:, cols],
                start=True,
                stop=True,
            )
            return acc

        halves = (low, high)

        def scratch(name, shape):
            place = PLACES.get(name, name)
            if isinstance(place, int):
                return shared.tile(shape, F32, name=name, offset=place)
            return keep.tile(shape, F32, name=name, tag=place)

        rows = {}
        own = [scratch("own%d" % t, [P, HALF]) for t in range(PAIR)]
        out_rows = out.rearrange("(p t) j -> p t j", t=TILES)
        fetched, turned, sigmoids, diffs, product, gains_turned, back = {}, {}, {}, {}, {}, {}, {}

        def fetch_tile(t, h):
            if (t, h) not in fetched:
                fetched[(t, h)] = scratch("fetched%d_%d" % (t, h), [P, SIDES, HALF])
            return fetched[(t, h)]

        def gather_fused(t, sides=(0, 1)):
            for side in sides:
                nc.vector.tensor_tensor(out=fetch_tile(t, 0)[:, side, :], in0=windows[t][:].indirect(entries(partners[side], low)), in1=own[t][:], op=ALU.subtract)
            diffs[t] = fetched[(t, 0)]

        def gather_plain(t, sides=(0, 1)):
            for side in sides:
                nc.vector.tensor_copy(out=fetch_tile(t, 0)[:, side, :], in_=windows[t][:].indirect(entries(partners[side], low)))

        def subtract(t):
            diffs[t] = scratch("diff%d" % t, [P, SIDES, HALF])
            for side in range(SIDES):
                nc.vector.tensor_tensor(out=diffs[t][:, side], in0=fetched[(t, 0)][:, side], in1=accs[t][:, low], op=ALU.subtract)

        def turn_own(t, h, bank):
            turned[(t, h)] = psum.tile([P, S], F32, name="turned%d_%d" % (t, h), tag=bank)
            for i in range(S // P):
                first = h * HALF + i // SIDES * P
                nc.tensor.matmul(out=turned[(t, h)][:, i * P : (i + 1) * P], lhsT=windows[t][:, first : first + P], rhs=ident[:], start=(i == 0), stop=False, is_transpose=True)

        def subtract_on_gpsimd(t):
            diffs[t] = scratch("diff%d" % t, [P, SIDES, HALF])
            nc.gpsimd.tensor_tensor(out=diffs[t][:], in0=fetched[(t, 0)][:], in1=windows[t][:, low].unsqueeze(1).to_broadcast([P, SIDES, HALF]), op=ALU.subtract)

        def gather_high(t, side, on_vector=False):
            minus = fetch_tile(t, 1)[:, side, :]
            looked_up = windows[t][:].indirect(entries(partners[side], high))
            if on_vector:
                nc.vector.tensor_scalar(out=minus, in0=looked_up, scalar1=-1.0, scalar2=0.0, op0=ALU.mult, op1=ALU.add)
            else:
                nc.scalar.activation(out=minus, in_=looked_up, func=ACT.Copy, scale=-1.0)

        def turn_fetched(t, side):
            for b in range(HALF // P):
                place = turned[(t, 1)][:, (b * SIDES + side) * P : (b * SIDES + side + 1) * P]
                nc.tensor.matmul(out=place, lhsT=fetched[(t, 1)][:, side, b * P : (b + 1) * P], rhs=ident[:], start=False, stop=(side == 1 and b == 1), is_transpose=True)

        def sigmoid_low(t):
            plain = scratch("sigmoid%d" % t, [P, SIDES, HALF])
            nc.scalar.activation(out=plain[:], in_=diffs[t][:], func=ACT.Sigmoid)
            sigmoids[(t, 0)] = plain[:]

        def sigmoid_turned(t, blocks=(0, 1)):
            sigmoids[(t, 1, blocks)] = scratch("sig_turned%d_%d" % (t, blocks[0]), [P, len(blocks) * SIDES * P])
            nc.scalar.activation(out=sigmoids[(t, 1, blocks)][:], in_=turned[(t, 1)][:, blocks[0] * SIDES * P : (blocks[-1] + 1) * SIDES * P], func=ACT.Sigmoid, scale=-1.0)

        def turn_sigmoids(t, bank):
            plain = psum.tile([P, SIDES, HALF], F32, name="sig_back%d" % t, tag=bank)
            for i in range(S // P):
                b, side = divmod(i, SIDES)
                nc.tensor.transpose(plain[:, side, b * P : (b + 1) * P], sigmoids[(t, 1, (0, 1))][:, i * P : (i + 1) * P], ident[:])
            sigmoids[(t, 1)] = plain[:]

        def turn_gains(t, bank):
            gains_turned[t] = psum.tile([P, S], F32, name="gains_turned%d" % t, tag=bank)
            for i in range(S // P):
                first = HALF + i // SIDES * P
                nc.tensor.transpose(gains_turned[t][:, i * P : (i + 1) * P], gains[t // PAIR][:, i % SIDES, t % PAIR, first : first + P], ident[:])

        def weigh_turned(t, blocks=(0, 1)):
            if (t, 1) not in product:
                product[(t, 1)] = scratch("product%d_1" % t, [P, S])
            cols = slice(blocks[0] * SIDES * P, (blocks[-1] + 1) * SIDES * P)
            nc.vector.tensor_tensor(out=product[(t, 1)][:, cols], in0=sigmoids[(t, 1, blocks)][:] if (t, 1, blocks) in sigmoids else sigmoids[(t, 1, (0, 1))][:, cols], in1=gains_turned[t][:, cols], op=ALU.mult)

        def turn_back(t, bank, blocks=(0, 1)):
            back[(t, blocks[0])] = psum.tile([P, len(blocks) * P], F32, name="back%d_%d" % (t, blocks[0]), tag=bank)
            for i, b in enumerate(blocks):
                for side in range(SIDES):
                    first = (b * SIDES + side) * P
                    nc.tensor.matmul(out=back[(t, blocks[0])][:, i * P : (i + 1) * P], lhsT=product[(t, 1)][:, first : first + P], rhs=ident[:], start=(side == 0), stop=(side == 1), is_transpose=True)

        def weigh_and_turn(t, bank):
            back[(t, 0)] = psum.tile([P, HALF], F32, name="back%d" % t, tag=bank)
            for b in range(HALF // P):
                weigh_turned(t, (b,))
                for side in range(SIDES):
                    first = (b * SIDES + side) * P
                    nc.tensor.matmul(out=back[(t, 0)][:, b * P : (b + 1) * P], lhsT=product[(t, 1)][:, first : first + P], rhs=ident[:], start=(side == 0), stop=(side == 1), is_transpose=True)

        def finish_turned(t, blocks=(0, 1), on_vector=False):
            summed = rows[t][:, HALF + blocks[0] * P : HALF + (blocks[-1] + 1) * P] if t in rows else scratch("result%d_1_%d" % (t, blocks[0]), [P, len(blocks) * P])
            if on_vector:
                nc.vector.tensor_copy(out=summed[:, :], in_=back[(t, blocks[0])][:])
            else:
                nc.scalar.copy(out=summed[:, :], in_=back[(t, blocks[0])][:])
            queue = nc.scalar if blocks == (1,) else nc.sync
            if t not in rows:
                queue.dma_start(out=out_rows[:, t, HALF + blocks[0] * P : HALF + (blocks[-1] + 1) * P], in_=summed[:])

        def weigh(t, h, engine=nc.vector):
            if (t, h) not in product:
                if (t, h) == (0, 0):
                    both = scratch("product_low", [P, PAIR, SIDES, HALF])
                    product[(0, 0)], product[(1, 0)], product["both"] = both[:, 0], both[:, 1], both
                else:
                    product[(t, h)] = scratch("product%d_%d" % (t, h), [P, SIDES, HALF])[:]
            engine.tensor_tensor(out=product[(t, h)], in0=sigmoids[(t, h)], in1=gains[t // PAIR][:, :, t % PAIR, halves[h]], op=ALU.mult)

        def finish_both(engine):
            summed = scratch("result_low", [P, PAIR, HALF])
            engine.tensor_tensor(out=summed[:], in0=product["both"][:, :, 0], in1=product["both"][:, :, 1], op=ALU.add)
            nc.sync.dma_start(out=out_rows[:, :PAIR, low], in_=summed[:])

        def finish(t, h, engine=nc.vector):
            summed = rows[t][:, halves[h]] if t in rows else scratch("result%d_%d" % (t, h), [P, HALF])[:]
            engine.tensor_tensor(out=summed, in0=product[(t, h)][:, 0], in1=product[(t, h)][:, 1], op=ALU.add)
            if t not in rows:
                nc.sync.dma_start(out=out_rows[:, t, halves[h]], in_=summed)

        def finish_last(t):
            made = scratch("product%d_0" % t, [P, SIDES, HALF])
            summed = rows[t] if t in rows else scratch("result%d_0" % t, [P, HALF])
            blocks = [slice(b * P, (b + 1) * P) for b in range(HALF // P)]
            for cols in blocks:
                nc.vector.tensor_tensor(out=made[:, :, cols], in0=sigmoids[(t, 0)][:, :, cols], in1=gains[t // PAIR][:, :, t % PAIR, cols], op=ALU.mult)
            for cols in blocks:
                nc.vector.tensor_tensor(out=summed[:, cols], in0=made[:, 0, cols], in1=made[:, 1, cols], op=ALU.add)
            if t not in rows:
                nc.sync.dma_start(out=out_rows[:, t, low], in_=summed[:])

        def open_row(t):
            rows[t] = scratch("row%d" % t, [P, S])

        def store_row(t):
            nc.sync.dma_start(out=out_rows[:, t, :], in_=rows[t][:])

        acc_low = [multiply(t, low, "bank%d" % t) for t in range(2)]
        acc_high = [multiply(t, high, "bank%d" % (2 + t)) for t in range(2)]
        accs = {t: multiply(t, whole, "bank%d" % (2 + t)) for t in (2, 3)}
        for t in range(2):
            nc.scalar.copy(out=windows[t][:, low], in_=acc_low[t][:])
            nc.vector.tensor_copy(out=own[t][:], in_=acc_low[t][:])
        for t in range(2):
            nc.scalar.copy(out=windows[t][:, high], in_=acc_high[t][:])

        def copy_scores(t):
            windows.append(scratch("window%d" % t, [P, S]))
            nc.vector.tensor_copy(out=windows[t][:], in_=accs[t][:])

        gather_fused(0)
        gather_high(0, 0)
        gather_high(0, 1)
        turn_own(0, 1, "bank6")
        turn_fetched(0, 0)
        turn_own(1, 1, "bank7")
        turn_fetched(0, 1)
        gather_fused(1)
        gather_high(1, 0)
        turn_fetched(1, 0)
        sigmoid_low(0)
        copy_scores(2)
        weigh(0, 0, nc.gpsimd)
        gather_high(1, 1)
        sigmoid_low(1)
        sigmoid_turned(0)
        turn_fetched(1, 1)
        turn_own(2, 1, "bank1")
        turn_sigmoids(0, "bank0")
        copy_scores(3)
        gather_plain(2)
        weigh(1, 0, nc.gpsimd)
        subtract(2)
        weigh(0, 1)
        finish_both(nc.gpsimd)
        finish(0, 1, nc.gpsimd)
        gather_high(2, 0)
        gather_high(2, 1)
        turn_fetched(2, 0)
        turn_own(3, 1, "bank3")
        turn_fetched(2, 1)
        gather_high(3, 0)
        gather_high(3, 1)
        turn_fetched(3, 0)
        turn_gains(1, "bank2")
        turn_fetched(3, 1)
        turn_gains(2, "bank6")
        turn_gains(3, "bank4")
        sigmoid_low(2)
        sigmoid_turned(1)
        gather_plain(3)
        subtract(3)
        weigh(2, 0, nc.gpsimd)
        sigmoid_turned(2)
        weigh_and_turn(1, "bank7")
        sigmoid_turned(3, (0,))
        sigmoid_turned(3, (1,))
        sigmoid_low(3)
        finish_turned(1)
        weigh_and_turn(2, "bank0")
        weigh_turned(3, (0,))
        turn_back(3, "bank1", (0,))
        weigh_turned(3, (1,))
        turn_back(3, "bank5", (1,))
        open_row(2)
        finish(2, 0)
        finish_turned(2)
        store_row(2)
        open_row(3)
        finish_turned(3, (0,))
        finish_last(3)
        finish_turned(3, (1,))
        store_row(3)
